import numpy as np
import ml_dtypes


def mxq(x, axis, fmt="e4m3"):
    dtype, down = {"e4m3": (ml_dtypes.float8_e4m3fn, 7), "e5m2": (ml_dtypes.float8_e5m2, 14)}[fmt]
    v = np.moveaxis(np.asarray(x, np.float32).astype(ml_dtypes.bfloat16).astype(np.float64), axis, -1)
    blocks = v.reshape(v.shape[:-1] + (-1, 32))
    amax = np.abs(blocks).max(-1, keepdims=True)
    byte = np.maximum(np.where(amax > 0, np.frexp(amax)[1] - 1 + 127, 0) - down, 1)
    scale = np.exp2(byte - 127.0)
    codes = (blocks / scale).astype(np.float32).astype(dtype).astype(np.float64)
    return np.moveaxis((codes * scale).reshape(v.shape), -1, axis)


WIDE = False


def mx_kscale(k):
    if not WIDE:
        return np.ones(k)
    levels = np.array([10, -10, 5, -5, 0])
    if k % 512:
        return np.exp2(np.random.permutation(np.resize(levels, k // 32))).repeat(32)
    a = np.empty((k // 512, 16))
    for p in range(k // 512):
        a[p, :8] = np.random.permutation(np.resize(levels, 8))
        for g in range(8):
            far = levels[np.abs(levels - a[p, g]) >= 10]
            a[p, g + 8] = far[np.random.randint(len(far))]
    return np.exp2(a.ravel()).repeat(32)


BF16 = ml_dtypes.bfloat16


def bf(x):
    return np.asarray(x, np.float32).astype(BF16)


def f64(x):
    return np.asarray(x).astype(np.float64)


E2M1 = np.array([0.0, 0.5, 1.0, 1.5, 2.0, 3.0, 4.0, 6.0, -0.0, -0.5, -1.0, -1.5, -2.0, -3.0, -4.0, -6.0])


def pack_weight(w, fmt):
    k, n = w.shape
    w = f64(bf(w)).reshape(k // 32, 32, n)
    amax = np.abs(w).max(1)
    if fmt == "e4m3":
        byte = np.frexp(amax)[1] - 1 + 127 - 7
    else:
        mant, ex = np.frexp(amax / 6.0)
        byte = np.where(mant > 0.5, ex, ex - 1) + 127
    byte = np.clip(np.where(amax > 0, byte, 1), 1, 254)
    scaled = (w * np.exp2(127.0 - byte)[:, None, :]).reshape(k, n).astype(np.float32)
    by_word = np.ascontiguousarray(scaled.reshape(k // 512, 128, 4, n).transpose(0, 1, 3, 2))
    if fmt == "e4m3":
        words = by_word.astype(ml_dtypes.float8_e4m3fn).view(np.uint8)
    else:
        c = by_word.astype(ml_dtypes.float4_e2m1fn).view(np.uint8) & 0xF
        words = c[..., 0::2] | (c[..., 1::2] << 4)
    return np.ascontiguousarray(words), np.ascontiguousarray(byte.astype(np.uint8).reshape(k // 512, 16, n))


def unpack_weight(words, scales, fmt):
    g, p, n, _ = words.shape
    if fmt == "e4m3":
        vals = np.ascontiguousarray(words).view(ml_dtypes.float8_e4m3fn).astype(np.float64)
    else:
        nib = np.empty((g, p, n, 4), np.uint8)
        nib[..., 0::2] = words & 0xF
        nib[..., 1::2] = words >> 4
        vals = E2M1[nib]
    vals = vals * np.repeat(np.exp2(scales.astype(np.float64) - 127.0), 8, axis=1)[..., None]
    return vals.transpose(0, 1, 3, 2).reshape(g * 512, n)
def pack4(w):
    words, scales = pack_weight(w, "e2m1")
    return words.reshape(words.shape[0], 128, -1), scales


def unpack4(words, scales):
    return unpack_weight(words.reshape(words.shape[0], 128, -1, 2), scales, "e2m1")


E4M3FN = np.array([(-1.0 if i & 128 else 1.0) * ((1.0 + (i & 7) / 8.0) * 2.0 ** (((i >> 3) & 15) - 7) if i & 120 else (i & 7) * 2.0 ** -9) for i in range(256)])


def e4m3fn_bytes(y):
    return np.clip(np.asarray(y, np.float64), -448.0, 448.0).astype(np.float32).astype(ml_dtypes.float8_e4m3fn).view(np.uint8)


def e4m3fn_values(b):
    return E4M3FN[b]


B, S, D, M, N, C = 2, 1024, 512, 512, 512, 2


def cauchy_parts(om, nu, b):
    de = om[:, None] - nu[None, :]
    w = b[None, :] / (0.25 + de * de)
    gr = 0.5 * w
    gi = -de * w
    return gr, gi


def draw0():
    s, t, r = mx_kscale(S), mx_kscale(M), mx_kscale(N)
    x = bf(np.random.standard_normal((B, S, D)) / s[None, :, None])
    p = np.random.standard_normal((M, S)) / np.sqrt(S) * s[None, :] * t[:, None]
    p_words, p_scales = pack4(p.T)
    om = bf(np.random.uniform(-4.0, 4.0, M))
    nu = bf(np.random.uniform(-4.0, 4.0, N))
    b = bf(np.random.standard_normal(N) * r)
    c = np.random.standard_normal((N, D)) * 1.5 / np.sqrt(N) / r[:, None]
    c_words, c_scales = pack4(c)
    q = bf(np.random.standard_normal((C, S, M)) / np.sqrt(M) / t[None, None, :])
    return {"x": x,
            "p_words": p_words,
            "p_scales": p_scales,
            "om": om,
            "nu": nu,
            "b": b,
            "c_words": c_words,
            "c_scales": c_scales,
            "q": q}


def core(x, p_words, p_scales, om, nu, b, c_words, c_scales, q):
    gr, gi = cauchy_parts(f64(om), f64(nu), f64(b))
    gr, gi = gr, gi
    cq = unpack4(c_words, c_scales)
    kr = mxq(gr, 1, "e4m3") @ cq
    ki = mxq(gi, 1, "e4m3") @ cq
    u = unpack4(p_words, p_scales).T @ mxq(f64(x), 1, "e4m3")
    fr = kr[None, :, :] * u
    fi = ki[None, :, :] * u
    qq = mxq(f64(q), 2, "e4m3")
    return (qq[0] @ mxq(fr, 1, "e4m3")) - (qq[1] @ mxq(fi, 1, "e4m3"))


def setup_inputs():
    drawn = draw0()
    full = np.asarray(drawn['x']).astype(np.float64)
    scale = (np.abs(full).reshape(2, 8, 128, 4, 128).max(axis=(2, 4)) / 448.0).astype(np.float32)
    given = {}
    for key, value in drawn.items():
        if key == 'x':
            given['x_bytes'] = e4m3fn_bytes(full / np.repeat(np.repeat(scale.astype(np.float64), 128, axis=1), 128, axis=2))
            given['x_scale'] = scale
        else:
            given[key] = value
    return given


def reference(x_bytes, x_scale, p_words, p_scales, om, nu, b, c_words, c_scales, q):
    return core(e4m3fn_values(x_bytes) * np.repeat(np.repeat(x_scale.astype(np.float64), 128, axis=1), 128, axis=2), p_words, p_scales, om, nu, b, c_words, c_scales, q)

@@ -1,0 +1,431 @@
+from contextlib import ExitStack
+
+import concourse.mybir as mybir
+from concourse.masks import make_identity
+
+F32 = mybir.dt.float32
+BF16 = mybir.dt.bfloat16
+U32 = mybir.dt.uint32
+I32 = mybir.dt.int32
+U8 = mybir.dt.uint8
+FP8 = mybir.dt.float8_e4m3fn
+E4M3 = mybir.dt.float8_e4m3fn_x4
+E2M1 = mybir.dt.float4_e2m1fn_x4
+MULT = mybir.AluOpType.mult
+ACT = mybir.ActivationFunctionType
+
+B, S, D, M, N = 2, 1024, 512, 512, 512
+P = 128
+T = 4
+RUN = 4
+BLOCKS = D // P
+ROW_TILES = S // P
+
+FLOPS = 2 * (2 * M * N * D + B * M * S * D + 2 * B * S * M * D)
+
+PIECES = ((0, 0, 2), (0, 2, 2), (1, 0, 2), (1, 2, 1), (1, 3, 1))
+
+
+def tile_cauchytransferfunctionfilter_d2p_kernel(
+    tc, x_bytes, x_scale, p_words, p_scales, om, nu, b, c_words, c_scales, q, out
+):
+    nc = tc.nc
+    with ExitStack() as ctx:
+        keep = ctx.enter_context(tc.tile_pool(name="keep", bufs=1))
+        psum = ctx.enter_context(tc.psum_pool(name="psum", bufs=8))
+        ctx.enter_context(tc.manual_schedule())
+
+        def bank(name):
+            return psum.tile([P, 512], F32, tag="bank", name=name)
+
+        def sb(name, shape, dt):
+            return keep.tile(shape, dt, name=name, align_bytes=64)
+
+        def cols(n, width=P):
+            return slice(width * n, width * n + width)
+
+        def by_runs(ap):
+            return ap.rearrange("p (t g i) -> p g t i", t=T, i=RUN)
+
+        def runs_of_words(ap):
+            return ap.rearrange("p (g i) t -> p g t i", i=RUN)
+
+        left = sb("left", [P, N], BF16)
+        right = sb("right", [P, M], BF16)
+        b_col = sb("b_col", [P, T], BF16)
+        squares = sb("squares", [P, T, M], F32)
+        roots = sb("roots", [P, T, M], F32)
+        w = sb("w", [P, T, M], F32)
+        g_bf = [sb("g_bf%d" % c, [P, M, T], BF16) for c in range(2)]
+        g_codes = [sb("g_codes%d" % c, [P, M], U32) for c in range(2)]
+        g_scales = [sb("g_scales%d" % c, [P, M], U8) for c in range(2)]
+
+        c_codes = sb("c_codes", [P, 2 * D], U8)
+        c_planes = sb("c_planes", [P, D], U8)
+        transfer_kept = sb("transfer_kept", [P, BLOCKS, 2, P // RUN, T, RUN], F32)
+
+        p_raw = sb("p_raw", [P, 2, 2 * M], U8)
+        p_raw_planes = sb("p_raw_planes", [P, 2, M], U8)
+        p_codes = sb("p_codes", [P, 2, 2 * M], U8)
+        p_planes = sb("p_planes", [P, 2, M], U8)
+
+        x_raw = [[sb("x_raw%d%d" % (i, g), [P, T, D], U8) for g in range(2)] for i in range(B)]
+        x_inter = [[sb("x_inter%d%d" % (i, g), [P, D, T], U8) for g in range(2)] for i in range(B)]
+        x_bf = [sb("x_bf%d" % i, [P, 2, D * T], BF16) for i in range(B)]
+        x_codes = [sb("x_codes%d" % i, [P, 2, D], U32) for i in range(B)]
+        x_planes = [sb("x_planes%d" % i, [P, 2, D], U8) for i in range(B)]
+        xs_rows = sb("xs_rows", [P, 32], F32)
+        xs_columns = sb("xs_columns", [P, 32], F32)
+        xs_spread = sb("xs_spread", [P, 32], F32)
+        x_s = sb("x_s", [P, 32], F32)
+
+        identity = sb("identity", [P, P], F32)
+        q_raw = sb("q_raw", [P, 2, ROW_TILES, M], BF16)
+        q_bf = [sb("q_bf%d" % h, [P, 2, 4, P, T], BF16) for h in range(2)]
+        q_codes = [sb("q_codes%d" % h, [P, 2, 4 * P], U32) for h in range(2)]
+        q_planes = [sb("q_planes%d" % h, [P, 2, 4 * P], U8) for h in range(2)]
+
+        f_bf = [sb("f_bf%d" % z, [P, 2, P * PIECES[z][2], T], BF16) for z in range(len(PIECES))]
+        f_codes = [sb("f_codes%d" % z, [P, 2, P * PIECES[z][2]], U32) for z in range(len(PIECES))]
+        f_planes = [sb("f_planes%d" % z, [P, 2, P * PIECES[z][2]], U8) for z in range(len(PIECES))]
+        o_sb = [sb("o_sb%d" % z, [P, ROW_TILES, P * PIECES[z][2]], F32) for z in range(len(PIECES))]
+
+        difference_bank, transfer_bank, q_bank, u_bank = {}, {}, {}, {}
+
+        nc.gpsimd.memset(xs_rows[:], 0.0)
+        nc.vector.memset(right[:], 0.0)
+        nc.gpsimd.memset(left[:], 1.0)
+        nc.vector.memset(right[32:33, :], -1.0)
+        warm_in = sb("warm_in", [P, 1], F32)
+        warm_out = sb("warm_out", [P, 1], F32)
+        nc.vector.memset(warm_in[:], 1.0)
+        nc.vector.memset(c_planes[:].bitcast(I32), 0)
+        nc.gpsimd.memset(p_raw_planes[:].rearrange("p g n -> p (g n)").bitcast(I32), 0)
+
+        def load_x(i, g):
+            nc.sync.dma_start(
+                out=x_raw[i][g][:], in_=x_bytes[i].rearrange("(g p t) d -> g p t d", p=P, t=T)[g]
+            )
+
+        def load_q(h, c):
+            nc.sync.dma_start(
+                out=q_raw[:, c, cols(h, 4), :],
+                in_=q[c].rearrange("(p j) m -> p j m", j=ROW_TILES)[:, cols(h, 4), :],
+            )
+
+        load_x(0, 0)
+        nc.sync.dma_start(out=right[0:1, :], in_=om.rearrange("(o m) -> o m", o=1))
+        nc.sync.dma_start(out=left[32:33, :], in_=nu.rearrange("(o n) -> o n", o=1))
+        nc.scalar.dma_start(
+            out=xs_rows[0:128:32, 0:16].rearrange("a (n j) -> a n j", j=BLOCKS),
+            in_=x_scale.rearrange("i (g a) j -> a (i g) j", a=4),
+        )
+        nc.scalar.dma_start(out=b_col[:], in_=b.rearrange("(p t) -> p t", t=T))
+        nc.scalar.activation(out=warm_out[:], in_=warm_in[:], func=ACT.Abs_reciprocal_sqrt)
+        load_x(0, 1)
+        load_x(1, 0)
+        load_x(1, 1)
+        nc.sync.dma_start(out=p_raw[:].bitcast(I32), in_=p_words.rearrange("g p n -> p g n").bitcast(I32))
+        load_q(0, 0)
+        load_q(0, 1)
+        load_q(1, 0)
+        nc.sync.dma_start(out=c_codes[:].bitcast(I32), in_=c_words[0].bitcast(I32))
+        for quad in range(4):
+            nc.sync.dma_start(
+                out=p_raw_planes[32 * quad : 32 * quad + 4, :, :].bitcast(I32),
+                in_=p_scales[:, cols(quad, 4), :].rearrange("g r n -> r g n").bitcast(I32),
+            )
+        for quad in range(4):
+            nc.sync.dma_start(
+                out=c_planes[32 * quad : 32 * quad + 4, :].bitcast(I32),
+                in_=c_scales[0, cols(quad, 4), :].bitcast(I32),
+            )
+        load_q(1, 1)
+        make_identity(nc, identity[:])
+
+        def difference(tm):
+            d = difference_bank[tm] = bank("difference%d" % tm)
+            for t in range(T):
+                nc.tensor.matmul(d[:, cols(t)], lhsT=left[:, t::T], rhs=right[:, tm::T], start=True, stop=True)
+
+        def square(tm):
+            nc.scalar.activation(
+                out=squares[:, :, cols(tm)],
+                in_=difference_bank[tm][:].rearrange("p (t m) -> p t m", t=T),
+                func=ACT.Square,
+            )
+
+        def inverse_root(half):
+            ms = cols(half, 2 * P)
+            nc.scalar.activation(
+                out=roots[:, :, ms], in_=squares[:, :, ms], func=ACT.Abs_reciprocal_sqrt, bias=0.25
+            )
+
+        def weight(t):
+            nc.vector.scalar_tensor_tensor(
+                out=w[:, t, :], in0=roots[:, t, :], scalar=b_col[:, t : t + 1], in1=roots[:, t, :], op0=MULT, op1=MULT
+            )
+
+        def g_imaginary(tm):
+            nc.vector.tensor_tensor(
+                out=runs_of_words(g_bf[1][:, cols(tm), :]),
+                in0=by_runs(difference_bank[tm][:]),
+                in1=w[:, :, cols(tm)].rearrange("p t (g i) -> p g t i", i=RUN),
+                op=MULT,
+            )
+
+        def g_real():
+            nc.vector.tensor_scalar(
+                out=runs_of_words(g_bf[0][:]),
+                in0=w[:].rearrange("p t (g i) -> p g t i", i=RUN),
+                scalar1=0.5,
+                scalar2=None,
+                op0=MULT,
+            )
+
+        def g_quantize(c):
+            nc.vector.quantize_mx(
+                out=g_codes[c][:].bitcast(E4M3), scales=g_scales[c][:], in_=g_bf[c][:].rearrange("p m t -> p (m t)")
+            )
+
+        def transfer(blk, c):
+            k_ps = transfer_bank[blk, c] = bank("transfer%d%d" % (blk, c))
+            for t in range(T):
+                nc.tensor.matmul_mx(
+                    out=k_ps[:, cols(t)],
+                    lhsT=g_codes[c][:, cols(t)].bitcast(E4M3),
+                    lhsT_scale=g_scales[c][:, cols(t)],
+                    rhs=c_codes[:, cols(blk, 2 * P)].bitcast(E2M1),
+                    rhs_scale=c_planes[:, cols(blk)],
+                    start=True,
+                    stop=True,
+                )
+
+        def keep_transfer(blk, c):
+            nc.scalar.copy(out=transfer_kept[:, blk, c], in_=by_runs(transfer_bank[blk, c][:]))
+
+        def permute_p_codes(g):
+            nc.vector.tensor_copy(
+                out=p_codes[:, g, :].rearrange("p (t n e) -> p t n e", t=T, e=2),
+                in_=p_raw[:, g, :].rearrange("p (n t e) -> p t n e", t=T, e=2),
+            )
+
+        def permute_p_planes():
+            nc.vector.tensor_copy(
+                out=p_planes[:].rearrange("p g (t n) -> p g t n", t=T),
+                in_=p_raw_planes[:].rearrange("p g (n t) -> p g t n", t=T),
+            )
+
+        def scales_to_columns():
+            nc.vector.transpose(out=xs_columns[:], in_=xs_rows[:])
+
+        def scales_repeat():
+            nc.vector.tensor_copy(out=xs_spread[:], in_=xs_columns[:, 0:1].to_broadcast([P, 32]))
+
+        def scales_to_rows():
+            nc.vector.transpose(out=x_s[:], in_=xs_spread[:])
+
+        def x_interleave(i, g):
+            nc.vector.tensor_copy(
+                out=runs_of_words(x_inter[i][g][:]), in_=x_raw[i][g][:].rearrange("p t (g i) -> p g t i", i=RUN)
+            )
+
+        def x_widen(i, g):
+            codes = x_inter[i][g][:].rearrange("p d t -> p (d t)")
+            for blk in range(BLOCKS):
+                ds = cols(blk, P * T)
+                column = BLOCKS * (2 * i + g) + blk
+                nc.scalar.activation(
+                    out=x_bf[i][:, g, ds],
+                    in_=codes[:, ds].bitcast(FP8),
+                    func=ACT.Copy,
+                    scale=x_s[:, column : column + 1],
+                )
+
+        def x_quantize(i):
+            nc.vector.quantize_mx(
+                out=x_codes[i][:].rearrange("p g d -> p (g d)").bitcast(E4M3),
+                scales=x_planes[i][:].rearrange("p g d -> p (g d)"),
+                in_=x_bf[i][:].rearrange("p g e -> p (g e)"),
+            )
+
+        def analysis(i, blk):
+            u_ps = u_bank[i, blk] = bank("u%d%d" % (i, blk))
+            for t in range(T):
+                for g in range(2):
+                    nc.tensor.matmul_mx(
+                        out=u_ps[:, cols(t)],
+                        lhsT=p_codes[:, g, cols(t, 2 * P)].bitcast(E2M1),
+                        lhsT_scale=p_planes[:, g, cols(t)],
+                        rhs=x_codes[i][:, g, cols(blk)].bitcast(E4M3),
+                        rhs_scale=x_planes[i][:, g, cols(blk)],
+                        start=(g == 0),
+                        stop=(g == 1),
+                    )
+
+        q_pairs = q_raw[:].rearrange("p c j m -> p (c j m)").bitcast(F32)
+
+        def q_turn(h, c):
+            for pair in range(2):
+                turned = q_bank[h, c, pair] = bank("turned%d%d%d" % (h, c, pair))
+                for s in range(2):
+                    first = (ROW_TILES * c + 4 * h + 2 * pair + s) * (M // 2)
+                    for u in range(2):
+                        nc.tensor.transpose(
+                            turned[:, cols(2 * s + u)], q_pairs[:, first + u : first + M // 2 : 2], identity[:]
+                        )
+
+        def q_copy(h, c):
+            for pair in range(2):
+                nc.scalar.copy(
+                    out=q_bf[h][:, c, cols(pair, 2)]
+                    .rearrange("p s r e -> p (s r e)")
+                    .bitcast(F32)
+                    .rearrange("p (s r u) -> p s r u", s=2, u=2),
+                    in_=q_bank[h, c, pair][:].rearrange("p (s u r) -> p s r u", s=2, u=2),
+                )
+
+        def q_quantize(h):
+            nc.vector.quantize_mx(
+                out=q_codes[h][:].rearrange("p c r -> p (c r)").bitcast(E4M3),
+                scales=q_planes[h][:].rearrange("p c r -> p (c r)"),
+                in_=q_bf[h][:].rearrange("p c s r e -> p (c s r e)"),
+            )
+
+        def filter_part(z, blk, c):
+            i, first = PIECES[z][:2]
+            nc.vector.tensor_tensor(
+                out=runs_of_words(f_bf[z][:, c, cols(blk - first), :]),
+                in0=by_runs(u_bank[i, blk][:]),
+                in1=transfer_kept[:, blk, c],
+                op=MULT,
+            )
+
+        def filter_block(z, blk):
+            for c in range(2):
+                filter_part(z, blk, c)
+
+        def f_quantize(z):
+            nc.vector.quantize_mx(
+                out=f_codes[z][:].rearrange("p c d -> p (c d)").bitcast(E4M3),
+                scales=f_planes[z][:].rearrange("p c d -> p (c d)"),
+                in_=f_bf[z][:].rearrange("p c d t -> p (c d t)"),
+            )
+
+        def synthesis(z, m, copy=nc.scalar.copy):
+            i, first, blocks = PIECES[z]
+            width = P * blocks
+            tiles = 512 // width
+            o_ps = bank("o%d%d" % (z, m))
+            for s in range(tiles):
+                j = tiles * m + s
+                for c in range(2):
+                    nc.tensor.matmul_mx(
+                        out=o_ps[:, cols(s, width)],
+                        lhsT=q_codes[j // 4][:, c, cols(j % 4)].bitcast(E4M3),
+                        lhsT_scale=q_planes[j // 4][:, c, cols(j % 4)],
+                        rhs=f_codes[z][:, c, :].bitcast(E4M3),
+                        rhs_scale=f_planes[z][:, c, :],
+                        start=(c == 0),
+                        stop=(c == 1),
+                    )
+            copy(out=o_sb[z][:, cols(m, tiles), :], in_=o_ps[:].rearrange("p (j d) -> p j d", d=width))
+            nc.sync.dma_start(
+                out=out[i].rearrange("(p j) d -> p j d", j=ROW_TILES)[
+                    :, cols(m, tiles), P * first : P * first + width
+                ],
+                in_=o_sb[z][:, cols(m, tiles), :],
+            )
+
+        for tm in range(T):
+            difference(tm)
+        for tm in range(T):
+            square(tm)
+        for half in range(2):
+            inverse_root(half)
+
+        x_interleave(0, 0)
+        scales_to_columns()
+        x_interleave(0, 1)
+        scales_repeat()
+        x_interleave(1, 0)
+        scales_to_rows()
+        x_interleave(1, 1)
+        permute_p_codes(0)
+        for t in range(T):
+            weight(t)
+        permute_p_codes(1)
+        for tm in range(T):
+            g_imaginary(tm)
+        g_real()
+
+        x_widen(0, 0)
+        x_widen(0, 1)
+        q_turn(0, 0)
+        q_turn(0, 1)
+        q_copy(0, 0)
+        q_copy(0, 1)
+        x_widen(1, 0)
+        q_turn(1, 0)
+
+        g_quantize(1)
+        permute_p_planes()
+        g_quantize(0)
+        x_quantize(0)
+        q_quantize(0)
+
+        for c in (1, 0):
+            for blk in (0, 1):
+                transfer(blk, c)
+                keep_transfer(blk, c)
+        analysis(0, 0)
+        analysis(0, 1)
+        x_widen(1, 1)
+        for c in (1, 0):
+            transfer(2, c)
+            keep_transfer(2, c)
+        q_turn(1, 1)
+        q_copy(1, 0)
+        q_copy(1, 1)
+        analysis(0, 2)
+        for c in (1, 0):
+            transfer(3, c)
+            keep_transfer(3, c)
+        analysis(0, 3)
+
+        filter_block(0, 0)
+        filter_block(0, 1)
+        f_quantize(0)
+        x_quantize(1)
+        filter_block(1, 2)
+        q_quantize(1)
+        filter_block(1, 3)
+
+        analysis(1, 0)
+        synthesis(0, 0)
+        synthesis(0, 1)
+        analysis(1, 1)
+        filter_part(2, 0, 0)
+        f_quantize(1)
+        filter_part(2, 0, 1)
+        filter_block(2, 1)
+        synthesis(0, 2)
+        synthesis(0, 3)
+        analysis(1, 2)
+        synthesis(1, 0)
+        synthesis(1, 1)
+        analysis(1, 3)
+        filter_part(3, 2, 0)
+        f_quantize(2)
+        filter_part(3, 2, 1)
+        filter_part(4, 3, 0)
+        f_quantize(3)
+        filter_part(4, 3, 1)
+        f_quantize(4)
+        synthesis(1, 2)
+        synthesis(1, 3)
+        for m in range(4):
+            synthesis(2, m)
+        for z in (3, 4):
+            synthesis(z, 0, nc.vector.tensor_copy)
+            synthesis(z, 1)

@@ -32,11 +32,14 @@ def tile_cauchytransferfunctionfilter_d2p_kernel(
     nc = tc.nc
     with ExitStack() as ctx:
         keep = ctx.enter_context(tc.tile_pool(name="keep", bufs=1))
-        psum = ctx.enter_context(tc.psum_pool(name="psum", bufs=8))
+        psum = ctx.enter_context(tc.psum_pool(name="psum", bufs=1))
         ctx.enter_context(tc.manual_schedule())
 
-        def bank(name):
-            return psum.tile([P, 512], F32, tag="bank", name=name)
+        def bank(n, name):
+            return psum.tile([P, 512], F32, tag="held%d" % n, name=name)
+
+        def passing_bank(name):
+            return psum.tile([P, 512], F32, tag="passing", name=name, bufs=4)
 
         def sb(name, shape, dt):
             return keep.tile(shape, dt, name=name, align_bytes=64)
@@ -70,10 +73,10 @@ def tile_cauchytransferfunctionfilter_d2p_kernel(
         p_planes = sb("p_planes", [P, 2, M], U8)
 
         x_raw = [[sb("x_raw%d%d" % (i, g), [P, T, D], U8) for g in range(2)] for i in range(B)]
-        x_inter = [[sb("x_inter%d%d" % (i, g), [P, D, T], U8) for g in range(2)] for i in range(B)]
-        x_bf = [sb("x_bf%d" % i, [P, 2, D * T], BF16) for i in range(B)]
-        x_codes = [sb("x_codes%d" % i, [P, 2, D], U32) for i in range(B)]
-        x_planes = [sb("x_planes%d" % i, [P, 2, D], U8) for i in range(B)]
+        x_wide = [[sb("x_wide%d%d" % (i, g), [P, T, D], BF16) for g in range(2)] for i in range(B)]
+        x_bf = [[sb("x_bf%d%d" % (i, h), [P, 2, 2 * P, T], BF16) for h in range(2)] for i in range(B)]
+        x_codes = [[sb("x_codes%d%d" % (i, h), [P, 2, 2 * P], U32) for h in range(2)] for i in range(B)]
+        x_planes = [[sb("x_planes%d%d" % (i, h), [P, 2, 2 * P], U8) for h in range(2)] for i in range(B)]
         xs_rows = sb("xs_rows", [P, 32], F32)
         xs_columns = sb("xs_columns", [P, 32], F32)
         xs_spread = sb("xs_spread", [P, 32], F32)
@@ -92,15 +95,16 @@ def tile_cauchytransferfunctionfilter_d2p_kernel(
 
         difference_bank, transfer_bank, q_bank, u_bank = {}, {}, {}, {}
 
-        nc.gpsimd.memset(xs_rows[:], 0.0)
-        nc.vector.memset(right[:], 0.0)
-        nc.gpsimd.memset(left[:], 1.0)
-        nc.vector.memset(right[32:33, :], -1.0)
+        nc.vector.memset(xs_rows[:], 0.0)
         warm_in = sb("warm_in", [P, 1], F32)
         warm_out = sb("warm_out", [P, 1], F32)
         nc.vector.memset(warm_in[:], 1.0)
+        nc.vector.memset(left[64:128, :], 1.0)
+        nc.vector.memset(right[0:127, :], -1.0)
+        nc.vector.memset(left[0:63, :], 0.0)
+        nc.vector.memset(left[64:127, :], 0.0)
+        nc.vector.memset(p_raw_planes[:].rearrange("p g n -> p (g n)").bitcast(I32), 0)
         nc.vector.memset(c_planes[:].bitcast(I32), 0)
-        nc.gpsimd.memset(p_raw_planes[:].rearrange("p g n -> p (g n)").bitcast(I32), 0)
 
         def load_x(i, g):
             nc.sync.dma_start(
@@ -113,38 +117,38 @@ def tile_cauchytransferfunctionfilter_d2p_kernel(
                 in_=q[c].rearrange("(p j) m -> p j m", j=ROW_TILES)[:, cols(h, 4), :],
             )
 
-        load_x(0, 0)
-        nc.sync.dma_start(out=right[0:1, :], in_=om.rearrange("(o m) -> o m", o=1))
-        nc.sync.dma_start(out=left[32:33, :], in_=nu.rearrange("(o n) -> o n", o=1))
-        nc.scalar.dma_start(
+        nc.sync.dma_start(out=right[127:128, :], in_=om.rearrange("(o m) -> o m", o=1))
+        nc.sync.dma_start(out=left[63:64, :], in_=nu.rearrange("(o n) -> o n", o=1))
+        nc.sync.dma_start(
             out=xs_rows[0:128:32, 0:16].rearrange("a (n j) -> a n j", j=BLOCKS),
             in_=x_scale.rearrange("i (g a) j -> a (i g) j", a=4),
         )
-        nc.scalar.dma_start(out=b_col[:], in_=b.rearrange("(p t) -> p t", t=T))
         nc.scalar.activation(out=warm_out[:], in_=warm_in[:], func=ACT.Abs_reciprocal_sqrt)
-        load_x(0, 1)
-        load_x(1, 0)
-        load_x(1, 1)
         nc.sync.dma_start(out=p_raw[:].bitcast(I32), in_=p_words.rearrange("g p n -> p g n").bitcast(I32))
+        load_x(0, 0)
+        load_x(0, 1)
+        nc.sync.dma_start(out=b_col[:], in_=b.rearrange("(p t) -> p t", t=T))
         load_q(0, 0)
-        load_q(0, 1)
-        load_q(1, 0)
-        nc.sync.dma_start(out=c_codes[:].bitcast(I32), in_=c_words[0].bitcast(I32))
         for quad in range(4):
             nc.sync.dma_start(
                 out=p_raw_planes[32 * quad : 32 * quad + 4, :, :].bitcast(I32),
                 in_=p_scales[:, cols(quad, 4), :].rearrange("g r n -> r g n").bitcast(I32),
             )
+        load_q(0, 1)
+        nc.sync.dma_start(out=c_codes[:].bitcast(I32), in_=c_words[0].bitcast(I32))
         for quad in range(4):
             nc.sync.dma_start(
                 out=c_planes[32 * quad : 32 * quad + 4, :].bitcast(I32),
                 in_=c_scales[0, cols(quad, 4), :].bitcast(I32),
             )
+        load_x(1, 0)
+        load_x(1, 1)
+        load_q(1, 0)
         load_q(1, 1)
         make_identity(nc, identity[:])
 
         def difference(tm):
-            d = difference_bank[tm] = bank("difference%d" % tm)
+            d = difference_bank[tm] = bank(tm, "difference%d" % tm)
             for t in range(T):
                 nc.tensor.matmul(d[:, cols(t)], lhsT=left[:, t::T], rhs=right[:, tm::T], start=True, stop=True)
 
@@ -161,10 +165,17 @@ def tile_cauchytransferfunctionfilter_d2p_kernel(
                 out=roots[:, :, ms], in_=squares[:, :, ms], func=ACT.Abs_reciprocal_sqrt, bias=0.25
             )
 
-        def weight(t):
-            nc.vector.scalar_tensor_tensor(
-                out=w[:, t, :], in0=roots[:, t, :], scalar=b_col[:, t : t + 1], in1=roots[:, t, :], op0=MULT, op1=MULT
-            )
+        def weight(half):
+            ms = cols(half, 2 * P)
+            for t in range(T):
+                nc.vector.scalar_tensor_tensor(
+                    out=w[:, t, ms],
+                    in0=roots[:, t, ms],
+                    scalar=b_col[:, t : t + 1],
+                    in1=roots[:, t, ms],
+                    op0=MULT,
+                    op1=MULT,
+                )
 
         def g_imaginary(tm):
             nc.vector.tensor_tensor(
@@ -174,13 +185,13 @@ def tile_cauchytransferfunctionfilter_d2p_kernel(
                 op=MULT,
             )
 
-        def g_real():
-            nc.vector.tensor_scalar(
-                out=runs_of_words(g_bf[0][:]),
-                in0=w[:].rearrange("p t (g i) -> p g t i", i=RUN),
-                scalar1=0.5,
-                scalar2=None,
-                op0=MULT,
+        def g_real(half):
+            ms = cols(half, 2 * P)
+            nc.scalar.activation(
+                out=runs_of_words(g_bf[0][:, ms, :]),
+                in_=w[:, :, ms].rearrange("p t (g i) -> p g t i", i=RUN),
+                func=ACT.Copy,
+                scale=0.5,
             )
 
         def g_quantize(c):
@@ -189,7 +200,7 @@ def tile_cauchytransferfunctionfilter_d2p_kernel(
             )
 
         def transfer(blk, c):
-            k_ps = transfer_bank[blk, c] = bank("transfer%d%d" % (blk, c))
+            k_ps = transfer_bank[blk, c] = passing_bank("transfer%d%d" % (blk, c))
             for t in range(T):
                 nc.tensor.matmul_mx(
                     out=k_ps[:, cols(t)],
@@ -225,40 +236,40 @@ def tile_cauchytransferfunctionfilter_d2p_kernel(
         def scales_to_rows():
             nc.vector.transpose(out=x_s[:], in_=xs_spread[:])
 
-        def x_interleave(i, g):
-            nc.vector.tensor_copy(
-                out=runs_of_words(x_inter[i][g][:]), in_=x_raw[i][g][:].rearrange("p t (g i) -> p g t i", i=RUN)
+        def x_widen(i, g, copy=nc.scalar.copy):
+            copy(
+                out=x_wide[i][g][:].rearrange("p t d -> p (t d)"),
+                in_=x_raw[i][g][:].rearrange("p t d -> p (t d)").bitcast(FP8),
             )
 
-        def x_widen(i, g):
-            codes = x_inter[i][g][:].rearrange("p d t -> p (d t)")
-            for blk in range(BLOCKS):
-                ds = cols(blk, P * T)
+        def x_scale(i, g, h, on_scalar=False):
+            for blk in (2 * h, 2 * h + 1):
                 column = BLOCKS * (2 * i + g) + blk
-                nc.scalar.activation(
-                    out=x_bf[i][:, g, ds],
-                    in_=codes[:, ds].bitcast(FP8),
-                    func=ACT.Copy,
-                    scale=x_s[:, column : column + 1],
-                )
+                scale = x_s[:, column : column + 1]
+                words = runs_of_words(x_bf[i][h][:, g, cols(blk % 2), :])
+                values = x_wide[i][g][:, :, cols(blk)].rearrange("p t (g i) -> p g t i", i=RUN)
+                if on_scalar:
+                    nc.scalar.activation(out=words, in_=values, func=ACT.Copy, scale=scale)
+                else:
+                    nc.vector.tensor_scalar(out=words, in0=values, scalar1=scale, scalar2=None, op0=MULT)
 
-        def x_quantize(i):
+        def x_quantize(i, h):
             nc.vector.quantize_mx(
-                out=x_codes[i][:].rearrange("p g d -> p (g d)").bitcast(E4M3),
-                scales=x_planes[i][:].rearrange("p g d -> p (g d)"),
-                in_=x_bf[i][:].rearrange("p g e -> p (g e)"),
+                out=x_codes[i][h][:].rearrange("p g d -> p (g d)").bitcast(E4M3),
+                scales=x_planes[i][h][:].rearrange("p g d -> p (g d)"),
+                in_=x_bf[i][h][:].rearrange("p g d t -> p (g d t)"),
             )
 
         def analysis(i, blk):
-            u_ps = u_bank[i, blk] = bank("u%d%d" % (i, blk))
+            u_ps = u_bank[i, blk] = bank(blk, "u%d%d" % (i, blk))
             for t in range(T):
                 for g in range(2):
                     nc.tensor.matmul_mx(
                         out=u_ps[:, cols(t)],
                         lhsT=p_codes[:, g, cols(t, 2 * P)].bitcast(E2M1),
                         lhsT_scale=p_planes[:, g, cols(t)],
-                        rhs=x_codes[i][:, g, cols(blk)].bitcast(E4M3),
-                        rhs_scale=x_planes[i][:, g, cols(blk)],
+                        rhs=x_codes[i][blk // 2][:, g, cols(blk % 2)].bitcast(E4M3),
+                        rhs_scale=x_planes[i][blk // 2][:, g, cols(blk % 2)],
                         start=(g == 0),
                         stop=(g == 1),
                     )
@@ -267,7 +278,7 @@ def tile_cauchytransferfunctionfilter_d2p_kernel(
 
         def q_turn(h, c):
             for pair in range(2):
-                turned = q_bank[h, c, pair] = bank("turned%d%d%d" % (h, c, pair))
+                turned = q_bank[h, c, pair] = passing_bank("turned%d%d%d" % (h, c, pair))
                 for s in range(2):
                     first = (ROW_TILES * c + 4 * h + 2 * pair + s) * (M // 2)
                     for u in range(2):
@@ -316,7 +327,8 @@ def tile_cauchytransferfunctionfilter_d2p_kernel(
             i, first, blocks = PIECES[z]
             width = P * blocks
             tiles = 512 // width
-            o_ps = bank("o%d%d" % (z, m))
+            name = "o%d%d" % (z, m)
+            o_ps = passing_bank(name) if blocks > 1 else bank(2 * (first % 2) + m, name)
             for s in range(tiles):
                 j = tiles * m + s
                 for c in range(2):
@@ -339,82 +351,87 @@ def tile_cauchytransferfunctionfilter_d2p_kernel(
 
         for tm in range(T):
             difference(tm)
-        for tm in range(T):
+        for tm in range(3):
             square(tm)
-        for half in range(2):
-            inverse_root(half)
-
-        x_interleave(0, 0)
-        scales_to_columns()
-        x_interleave(0, 1)
-        scales_repeat()
-        x_interleave(1, 0)
-        scales_to_rows()
-        x_interleave(1, 1)
-        permute_p_codes(0)
-        for t in range(T):
-            weight(t)
-        permute_p_codes(1)
-        for tm in range(T):
-            g_imaginary(tm)
-        g_real()
-
-        x_widen(0, 0)
+        inverse_root(0)
+        square(3)
         x_widen(0, 1)
+        inverse_root(1)
+
+        scales_to_columns()
+        permute_p_codes(0)
+        scales_repeat()
+        permute_p_codes(1)
+        scales_to_rows()
+        x_widen(0, 0, nc.vector.tensor_copy)
+        weight(0)
+        x_scale(0, 0, 0)
+        x_scale(0, 0, 1)
+        permute_p_planes()
+        weight(1)
         q_turn(0, 0)
         q_turn(0, 1)
-        q_copy(0, 0)
-        q_copy(0, 1)
+        for half in range(2):
+            g_real(half)
+            q_copy(0, half)
         x_widen(1, 0)
-        q_turn(1, 0)
-
+        x_widen(1, 1)
+        for tm in range(T):
+            g_imaginary(tm)
+        x_scale(0, 1, 0)
         g_quantize(1)
-        permute_p_planes()
+        x_quantize(0, 0)
         g_quantize(0)
-        x_quantize(0)
         q_quantize(0)
 
+        for blk in (0, 1):
+            transfer(blk, 1)
+            keep_transfer(blk, 1)
+        analysis(0, 0)
+        for blk in (0, 1):
+            transfer(blk, 0)
+            keep_transfer(blk, 0)
+        analysis(0, 1)
+        for c in range(2):
+            q_turn(1, c)
+            q_copy(1, c)
         for c in (1, 0):
-            for blk in (0, 1):
+            for blk in (2, 3):
                 transfer(blk, c)
                 keep_transfer(blk, c)
-        analysis(0, 0)
-        analysis(0, 1)
-        x_widen(1, 1)
-        for c in (1, 0):
-            transfer(2, c)
-            keep_transfer(2, c)
-        q_turn(1, 1)
-        q_copy(1, 0)
-        q_copy(1, 1)
-        analysis(0, 2)
-        for c in (1, 0):
-            transfer(3, c)
-            keep_transfer(3, c)
-        analysis(0, 3)
 
-        filter_block(0, 0)
+        x_scale(0, 1, 1)
+        filter_part(0, 0, 1)
+        x_quantize(0, 1)
+        filter_part(0, 0, 0)
         filter_block(0, 1)
+        x_scale(1, 0, 0)
         f_quantize(0)
-        x_quantize(1)
-        filter_block(1, 2)
+        x_scale(1, 1, 0)
         q_quantize(1)
-        filter_block(1, 3)
-
+        analysis(0, 2)
+        analysis(0, 3)
+        x_scale(1, 0, 1, on_scalar=True)
+        x_scale(1, 1, 1, on_scalar=True)
+        for m in range(4):
+            synthesis(0, m)
+        filter_part(1, 2, 1)
+        x_quantize(1, 0)
         analysis(1, 0)
-        synthesis(0, 0)
-        synthesis(0, 1)
         analysis(1, 1)
-        filter_part(2, 0, 0)
+        filter_part(1, 3, 1)
+        filter_part(1, 2, 0)
+        filter_part(1, 3, 0)
+        x_quantize(1, 1)
         f_quantize(1)
-        filter_part(2, 0, 1)
-        filter_block(2, 1)
-        synthesis(0, 2)
-        synthesis(0, 3)
         analysis(1, 2)
         synthesis(1, 0)
         synthesis(1, 1)
         analysis(1, 3)
+        synthesis(1, 2)
+        synthesis(1, 3)
+        filter_block(2, 0)
+        filter_block(2, 1)
         filter_part(3, 2, 0)
         f_quantize(2)
         filter_part(3, 2, 1)
@@ -422,8 +439,6 @@ def tile_cauchytransferfunctionfilter_d2p_kernel(
         f_quantize(3)
         filter_part(4, 3, 1)
         f_quantize(4)
-        synthesis(1, 2)
-        synthesis(1, 3)
         for m in range(4):
             synthesis(2, m)
         for z in (3, 4):

@@ -23,7 +23,7 @@ ROW_TILES = S // P
 
 FLOPS = 2 * (2 * M * N * D + B * M * S * D + 2 * B * S * M * D)
 
-PIECES = ((0, 0, 2), (0, 2, 2), (1, 0, 2), (1, 2, 1), (1, 3, 1))
+PIECES = ((0, 0, 2), (0, 2, 2), (1, 0, 2), (1, 2, 2))
 
 
 def tile_cauchytransferfunctionfilter_d2p_kernel(
@@ -50,6 +50,9 @@ def tile_cauchytransferfunctionfilter_d2p_kernel(
         def by_runs(ap):
             return ap.rearrange("p (t g i) -> p g t i", t=T, i=RUN)
 
+        def by_words(ap):
+            return ap.rearrange("p (t d) -> p d t", t=T)
+
         def runs_of_words(ap):
             return ap.rearrange("p (g i) t -> p g t i", i=RUN)
 
@@ -65,7 +68,7 @@ def tile_cauchytransferfunctionfilter_d2p_kernel(
 
         c_codes = sb("c_codes", [P, 2 * D], U8)
         c_planes = sb("c_planes", [P, D], U8)
-        transfer_kept = sb("transfer_kept", [P, BLOCKS, 2, P // RUN, T, RUN], F32)
+        transfer_kept = sb("transfer_kept", [P, BLOCKS, 2, P, T], F32)
 
         p_raw = sb("p_raw", [P, 2, 2 * M], U8)
         p_raw_planes = sb("p_raw_planes", [P, 2, M], U8)
@@ -213,7 +216,7 @@ def tile_cauchytransferfunctionfilter_d2p_kernel(
                 )
 
         def keep_transfer(blk, c):
-            nc.scalar.copy(out=transfer_kept[:, blk, c], in_=by_runs(transfer_bank[blk, c][:]))
+            nc.scalar.copy(out=transfer_kept[:, blk, c], in_=by_words(transfer_bank[blk, c][:]))
 
         def permute_p_codes(g):
             nc.vector.tensor_copy(
@@ -306,8 +309,8 @@ def tile_cauchytransferfunctionfilter_d2p_kernel(
         def filter_part(z, blk, c):
             i, first = PIECES[z][:2]
             nc.vector.tensor_tensor(
-                out=runs_of_words(f_bf[z][:, c, cols(blk - first), :]),
-                in0=by_runs(u_bank[i, blk][:]),
+                out=f_bf[z][:, c, cols(blk - first), :],
+                in0=by_words(u_bank[i, blk][:]),
                 in1=transfer_kept[:, blk, c],
                 op=MULT,
             )
@@ -328,7 +331,7 @@ def tile_cauchytransferfunctionfilter_d2p_kernel(
             width = P * blocks
             tiles = 512 // width
             name = "o%d%d" % (z, m)
-            o_ps = passing_bank(name) if blocks > 1 else bank(2 * (first % 2) + m, name)
+            o_ps = passing_bank(name) if z < 3 else bank(m, name)
             for s in range(tiles):
                 j = tiles * m + s
                 for c in range(2):
@@ -355,8 +358,8 @@ def tile_cauchytransferfunctionfilter_d2p_kernel(
             square(tm)
         inverse_root(0)
         square(3)
-        x_widen(0, 1)
         inverse_root(1)
+        x_widen(0, 1)
 
         scales_to_columns()
         permute_p_codes(0)
@@ -364,83 +367,73 @@ def tile_cauchytransferfunctionfilter_d2p_kernel(
         permute_p_codes(1)
         scales_to_rows()
         x_widen(0, 0, nc.vector.tensor_copy)
-        weight(0)
         x_scale(0, 0, 0)
+        weight(0)
         x_scale(0, 0, 1)
         permute_p_planes()
         weight(1)
         q_turn(0, 0)
         q_turn(0, 1)
-        for half in range(2):
-            g_real(half)
-            q_copy(0, half)
-        x_widen(1, 0)
-        x_widen(1, 1)
-        for tm in range(T):
-            g_imaginary(tm)
+        q_copy(0, 0)
+        q_copy(0, 1)
+        g_real(0)
+        g_real(1)
         x_scale(0, 1, 0)
-        g_quantize(1)
+        g_imaginary(0)
         x_quantize(0, 0)
+        for tm in range(1, T):
+            g_imaginary(tm)
         g_quantize(0)
+        g_quantize(1)
+        x_scale(0, 1, 1)
         q_quantize(0)
+        x_quantize(0, 1)
 
-        for blk in (0, 1):
-            transfer(blk, 1)
-            keep_transfer(blk, 1)
-        analysis(0, 0)
-        for blk in (0, 1):
-            transfer(blk, 0)
-            keep_transfer(blk, 0)
-        analysis(0, 1)
         for c in range(2):
             q_turn(1, c)
             q_copy(1, c)
-        for c in (1, 0):
-            for blk in (2, 3):
+        x_widen(1, 0)
+        for blk in range(BLOCKS):
+            if blk < 2:
+                analysis(0, blk)
+            for c in range(2):
                 transfer(blk, c)
                 keep_transfer(blk, c)
-
-        x_scale(0, 1, 1)
-        filter_part(0, 0, 1)
-        x_quantize(0, 1)
-        filter_part(0, 0, 0)
-        filter_block(0, 1)
-        x_scale(1, 0, 0)
-        f_quantize(0)
-        x_scale(1, 1, 0)
-        q_quantize(1)
+            if blk == 1:
+                x_widen(1, 1)
         analysis(0, 2)
         analysis(0, 3)
+
+        filter_block(0, 0)
+        filter_block(0, 1)
+        q_quantize(1)
+        f_quantize(0)
+        x_scale(1, 0, 0)
+        x_scale(1, 1, 0)
         x_scale(1, 0, 1, on_scalar=True)
         x_scale(1, 1, 1, on_scalar=True)
         for m in range(4):
             synthesis(0, m)
-        filter_part(1, 2, 1)
+        filter_part(1, 2, 0)
         x_quantize(1, 0)
         analysis(1, 0)
         analysis(1, 1)
-        filter_part(1, 3, 1)
-        filter_part(1, 2, 0)
-        filter_part(1, 3, 0)
+        filter_part(1, 2, 1)
+        filter_block(1, 3)
         x_quantize(1, 1)
         f_quantize(1)
         analysis(1, 2)
-        synthesis(1, 0)
-        synthesis(1, 1)
+        for m in range(4):
+            synthesis(1, m)
         analysis(1, 3)
-        synthesis(1, 2)
-        synthesis(1, 3)
         filter_block(2, 0)
         filter_block(2, 1)
         filter_part(3, 2, 0)
         f_quantize(2)
         filter_part(3, 2, 1)
-        filter_part(4, 3, 0)
+        filter_block(3, 3)
         f_quantize(3)
-        filter_part(4, 3, 1)
-        f_quantize(4)
         for m in range(4):
             synthesis(2, m)
-        for z in (3, 4):
-            synthesis(z, 0, nc.vector.tensor_copy)
-            synthesis(z, 1)
+        for m in range(4):
+            synthesis(3, m, nc.vector.tensor_copy if m % 2 == 0 else nc.scalar.copy)

@@ -12,6 +12,7 @@ FP8 = mybir.dt.float8_e4m3fn
 E4M3 = mybir.dt.float8_e4m3fn_x4
 E2M1 = mybir.dt.float4_e2m1fn_x4
 MULT = mybir.AluOpType.mult
+ADD = mybir.AluOpType.add
 ACT = mybir.ActivationFunctionType
 
 B, S, D, M, N = 2, 1024, 512, 512, 512
@@ -127,17 +128,19 @@ def tile_cauchytransferfunctionfilter_d2p_kernel(
             in_=x_scale.rearrange("i (g a) j -> a (i g) j", a=4),
         )
         nc.scalar.activation(out=warm_out[:], in_=warm_in[:], func=ACT.Abs_reciprocal_sqrt)
-        nc.sync.dma_start(out=p_raw[:].bitcast(I32), in_=p_words.rearrange("g p n -> p g n").bitcast(I32))
         load_x(0, 0)
+        nc.sync.dma_start(out=p_raw[:].bitcast(I32), in_=p_words.rearrange("g p n -> p g n").bitcast(I32))
         load_x(0, 1)
         nc.sync.dma_start(out=b_col[:], in_=b.rearrange("(p t) -> p t", t=T))
         load_q(0, 0)
+        load_q(0, 1)
         for quad in range(4):
             nc.sync.dma_start(
                 out=p_raw_planes[32 * quad : 32 * quad + 4, :, :].bitcast(I32),
                 in_=p_scales[:, cols(quad, 4), :].rearrange("g r n -> r g n").bitcast(I32),
             )
-        load_q(0, 1)
+        load_q(1, 0)
+        load_q(1, 1)
         nc.sync.dma_start(out=c_codes[:].bitcast(I32), in_=c_words[0].bitcast(I32))
         for quad in range(4):
             nc.sync.dma_start(
@@ -146,12 +149,11 @@ def tile_cauchytransferfunctionfilter_d2p_kernel(
             )
         load_x(1, 0)
         load_x(1, 1)
-        load_q(1, 0)
-        load_q(1, 1)
         make_identity(nc, identity[:])
 
-        def difference(tm):
-            d = difference_bank[tm] = bank(tm, "difference%d" % tm)
+        def difference(tm, held):
+            name = "difference%d%d" % (held, tm)
+            d = difference_bank[tm] = bank(tm, name) if held else passing_bank(name)
             for t in range(T):
                 nc.tensor.matmul(d[:, cols(t)], lhsT=left[:, t::T], rhs=right[:, tm::T], start=True, stop=True)
 
@@ -188,14 +190,24 @@ def tile_cauchytransferfunctionfilter_d2p_kernel(
                 op=MULT,
             )
 
-        def g_real(half):
+        def g_real(half, engine=None):
             ms = cols(half, 2 * P)
-            nc.scalar.activation(
-                out=runs_of_words(g_bf[0][:, ms, :]),
-                in_=w[:, :, ms].rearrange("p t (g i) -> p g t i", i=RUN),
-                func=ACT.Copy,
-                scale=0.5,
-            )
+            if engine:
+                engine.tensor_scalar(
+                    out=g_bf[0][:, ms, :],
+                    in0=w[:, :, ms].rearrange("p t m -> p m t"),
+                    scalar1=0.5,
+                    scalar2=0.0,
+                    op0=MULT,
+                    op1=ADD,
+                )
+            else:
+                nc.scalar.activation(
+                    out=runs_of_words(g_bf[0][:, ms, :]),
+                    in_=w[:, :, ms].rearrange("p t (g i) -> p g t i", i=RUN),
+                    func=ACT.Copy,
+                    scale=0.5,
+                )
 
         def g_quantize(c):
             nc.vector.quantize_mx(
@@ -281,7 +293,8 @@ def tile_cauchytransferfunctionfilter_d2p_kernel(
 
         def q_turn(h, c):
             for pair in range(2):
-                turned = q_bank[h, c, pair] = passing_bank("turned%d%d%d" % (h, c, pair))
+                name = "turned%d%d%d" % (h, c, pair)
+                turned = q_bank[h, c, pair] = passing_bank(name) if h else bank(2 * c + pair, name)
                 for s in range(2):
                     first = (ROW_TILES * c + 4 * h + 2 * pair + s) * (M // 2)
                     for u in range(2):
@@ -353,49 +366,51 @@ def tile_cauchytransferfunctionfilter_d2p_kernel(
             )
 
         for tm in range(T):
-            difference(tm)
-        for tm in range(3):
+            difference(tm, False)
+        x_widen(0, 0)
+        square(0)
+        x_widen(0, 1)
+        for tm in range(1, T):
             square(tm)
         inverse_root(0)
-        square(3)
         inverse_root(1)
-        x_widen(0, 1)
 
         scales_to_columns()
-        permute_p_codes(0)
         scales_repeat()
-        permute_p_codes(1)
         scales_to_rows()
-        x_widen(0, 0, nc.vector.tensor_copy)
-        x_scale(0, 0, 0)
-        weight(0)
-        x_scale(0, 0, 1)
+        permute_p_codes(0)
+        permute_p_codes(1)
+        for g in range(2):
+            for h in range(2):
+                x_scale(0, g, h)
+        x_quantize(0, 0)
+        x_quantize(0, 1)
         permute_p_planes()
+        weight(0)
         weight(1)
         q_turn(0, 0)
         q_turn(0, 1)
+        q_turn(1, 0)
         q_copy(0, 0)
         q_copy(0, 1)
+        for tm in range(T):
+            difference(tm, True)
+        q_turn(1, 1)
         g_real(0)
-        g_real(1)
-        x_scale(0, 1, 0)
-        g_imaginary(0)
-        x_quantize(0, 0)
-        for tm in range(1, T):
+        g_real(1, nc.gpsimd)
+        for c in range(2):
+            q_copy(1, c)
+        for tm in range(T):
             g_imaginary(tm)
         g_quantize(0)
         g_quantize(1)
-        x_scale(0, 1, 1)
         q_quantize(0)
-        x_quantize(0, 1)
+        q_quantize(1)
 
-        for c in range(2):
-            q_turn(1, c)
-            q_copy(1, c)
         x_widen(1, 0)
+        analysis(0, 0)
+        analysis(0, 1)
         for blk in range(BLOCKS):
-            if blk < 2:
-                analysis(0, blk)
             for c in range(2):
                 transfer(blk, c)
                 keep_transfer(blk, c)
@@ -406,9 +421,8 @@ def tile_cauchytransferfunctionfilter_d2p_kernel(
 
         filter_block(0, 0)
         filter_block(0, 1)
-        q_quantize(1)
-        f_quantize(0)
         x_scale(1, 0, 0)
+        f_quantize(0)
         x_scale(1, 1, 0)
         x_scale(1, 0, 1, on_scalar=True)
         x_scale(1, 1, 1, on_scalar=True)

@@ -97,7 +97,7 @@ def tile_cauchytransferfunctionfilter_d2p_kernel(
         f_planes = [sb("f_planes%d" % z, [P, 2, P * PIECES[z][2]], U8) for z in range(len(PIECES))]
         o_sb = [sb("o_sb%d" % z, [P, ROW_TILES, P * PIECES[z][2]], F32) for z in range(len(PIECES))]
 
-        difference_bank, transfer_bank, q_bank, u_bank = {}, {}, {}, {}
+        difference_bank, transfer_bank, q_bank, u_bank, out_bank = {}, {}, {}, {}, {}
 
         nc.vector.memset(xs_rows[:], 0.0)
         warm_in = sb("warm_in", [P, 1], F32)
@@ -251,10 +251,10 @@ def tile_cauchytransferfunctionfilter_d2p_kernel(
         def scales_to_rows():
             nc.vector.transpose(out=x_s[:], in_=xs_spread[:])
 
-        def x_widen(i, g, copy=nc.scalar.copy):
+        def x_widen(i, g, part=slice(0, T * D), copy=nc.scalar.copy):
             copy(
-                out=x_wide[i][g][:].rearrange("p t d -> p (t d)"),
-                in_=x_raw[i][g][:].rearrange("p t d -> p (t d)").bitcast(FP8),
+                out=x_wide[i][g][:].rearrange("p t d -> p (t d)")[:, part],
+                in_=x_raw[i][g][:].rearrange("p t d -> p (t d)")[:, part].bitcast(FP8),
             )
 
         def x_scale(i, g, h, on_scalar=False):
@@ -339,12 +339,19 @@ def tile_cauchytransferfunctionfilter_d2p_kernel(
                 in_=f_bf[z][:].rearrange("p c d t -> p (c d t)"),
             )
 
-        def synthesis(z, m, copy=nc.scalar.copy):
+        def f_quantize_part(z, c):
+            nc.vector.quantize_mx(
+                out=f_codes[z][:, c, :].bitcast(E4M3),
+                scales=f_planes[z][:, c, :],
+                in_=f_bf[z][:, c].rearrange("p d t -> p (d t)"),
+            )
+
+        def synthesis(z, m):
             i, first, blocks = PIECES[z]
             width = P * blocks
             tiles = 512 // width
             name = "o%d%d" % (z, m)
-            o_ps = passing_bank(name) if z < 3 else bank(m, name)
+            o_ps = out_bank[z, m] = passing_bank(name) if z < 3 else bank(m, name)
             for s in range(tiles):
                 j = tiles * m + s
                 for c in range(2):
@@ -357,7 +364,12 @@ def tile_cauchytransferfunctionfilter_d2p_kernel(
                         start=(c == 0),
                         stop=(c == 1),
                     )
-            copy(out=o_sb[z][:, cols(m, tiles), :], in_=o_ps[:].rearrange("p (j d) -> p j d", d=width))
+
+        def store(z, m, copy=nc.scalar.copy):
+            i, first, blocks = PIECES[z]
+            width = P * blocks
+            tiles = 512 // width
+            copy(out=o_sb[z][:, cols(m, tiles), :], in_=out_bank[z, m][:].rearrange("p (j d) -> p j d", d=width))
             nc.sync.dma_start(
                 out=out[i].rearrange("(p j) d -> p j d", j=ROW_TILES)[
                     :, cols(m, tiles), P * first : P * first + width
@@ -367,7 +379,7 @@ def tile_cauchytransferfunctionfilter_d2p_kernel(
 
         for tm in range(T):
             difference(tm, False)
-        x_widen(0, 0)
+        x_widen(0, 0, cols(1, 2 * D))
         square(0)
         x_widen(0, 1)
         for tm in range(1, T):
@@ -377,6 +389,7 @@ def tile_cauchytransferfunctionfilter_d2p_kernel(
 
         scales_to_columns()
         scales_repeat()
+        x_widen(0, 0, cols(0, 2 * D), nc.vector.tensor_copy)
         scales_to_rows()
         permute_p_codes(0)
         permute_p_codes(1)
@@ -384,7 +397,6 @@ def tile_cauchytransferfunctionfilter_d2p_kernel(
             for h in range(2):
                 x_scale(0, g, h)
         x_quantize(0, 0)
-        x_quantize(0, 1)
         permute_p_planes()
         weight(0)
         weight(1)
@@ -402,6 +414,7 @@ def tile_cauchytransferfunctionfilter_d2p_kernel(
             q_copy(1, c)
         for tm in range(T):
             g_imaginary(tm)
+        x_quantize(0, 1)
         g_quantize(0)
         g_quantize(1)
         q_quantize(0)
@@ -428,6 +441,7 @@ def tile_cauchytransferfunctionfilter_d2p_kernel(
         x_scale(1, 1, 1, on_scalar=True)
         for m in range(4):
             synthesis(0, m)
+            store(0, m)
         filter_part(1, 2, 0)
         x_quantize(1, 0)
         analysis(1, 0)
@@ -439,15 +453,19 @@ def tile_cauchytransferfunctionfilter_d2p_kernel(
         analysis(1, 2)
         for m in range(4):
             synthesis(1, m)
+            store(1, m)
         analysis(1, 3)
         filter_block(2, 0)
         filter_block(2, 1)
-        filter_part(3, 2, 0)
-        f_quantize(2)
-        filter_part(3, 2, 1)
+        f_quantize_part(2, 0)
+        f_quantize_part(2, 1)
+        filter_block(3, 2)
         filter_block(3, 3)
-        f_quantize(3)
+        f_quantize_part(3, 0)
+        f_quantize_part(3, 1)
         for m in range(4):
             synthesis(2, m)
+            store(2, m)
         for m in range(4):
-            synthesis(3, m, nc.vector.tensor_copy if m % 2 == 0 else nc.scalar.copy)
+            synthesis(3, m)
+            store(3, m, nc.vector.tensor_copy if m % 2 == 0 else nc.scalar.copy)

@@ -7,6 +7,7 @@ F32 = mybir.dt.float32
 BF16 = mybir.dt.bfloat16
 U32 = mybir.dt.uint32
 I32 = mybir.dt.int32
+U16 = mybir.dt.uint16
 U8 = mybir.dt.uint8
 FP8 = mybir.dt.float8_e4m3fn
 E4M3 = mybir.dt.float8_e4m3fn_x4
@@ -37,10 +38,13 @@ def tile_cauchytransferfunctionfilter_d2p_kernel(
         ctx.enter_context(tc.manual_schedule())
 
         def bank(n, name):
-            return psum.tile([P, 512], F32, tag="held%d" % n, name=name)
+            return psum.tile([P, 512], F32, tag="bank%d" % n, name=name)
+
+        passed = []
 
         def passing_bank(name):
-            return psum.tile([P, 512], F32, tag="passing", name=name, bufs=4)
+            passed.append(name)
+            return bank(4 + (len(passed) - 1) % 4, name)
 
         def sb(name, shape, dt):
             return keep.tile(shape, dt, name=name, align_bytes=64)
@@ -151,9 +155,8 @@ def tile_cauchytransferfunctionfilter_d2p_kernel(
         load_x(1, 1)
         make_identity(nc, identity[:])
 
-        def difference(tm, held):
-            name = "difference%d%d" % (held, tm)
-            d = difference_bank[tm] = bank(tm, name) if held else passing_bank(name)
+        def difference(tm, n):
+            d = difference_bank[tm] = bank(n, "difference%d%d" % (tm, n))
             for t in range(T):
                 nc.tensor.matmul(d[:, cols(t)], lhsT=left[:, t::T], rhs=right[:, tm::T], start=True, stop=True)
 
@@ -230,10 +233,10 @@ def tile_cauchytransferfunctionfilter_d2p_kernel(
         def keep_transfer(blk, c):
             nc.scalar.copy(out=transfer_kept[:, blk, c], in_=by_words(transfer_bank[blk, c][:]))
 
-        def permute_p_codes(g):
+        def permute_p_codes():
             nc.vector.tensor_copy(
-                out=p_codes[:, g, :].rearrange("p (t n e) -> p t n e", t=T, e=2),
-                in_=p_raw[:, g, :].rearrange("p (n t e) -> p t n e", t=T, e=2),
+                out=p_codes[:].bitcast(U16).rearrange("p g (t n) -> p g t n", t=T),
+                in_=p_raw[:].bitcast(U16).rearrange("p g (n t) -> p g t n", t=T),
             )
 
         def permute_p_planes():
@@ -291,10 +294,10 @@ def tile_cauchytransferfunctionfilter_d2p_kernel(
 
         q_pairs = q_raw[:].rearrange("p c j m -> p (c j m)").bitcast(F32)
 
-        def q_turn(h, c):
+        def q_turn(h, c, n):
             for pair in range(2):
                 name = "turned%d%d%d" % (h, c, pair)
-                turned = q_bank[h, c, pair] = passing_bank(name) if h else bank(2 * c + pair, name)
+                turned = q_bank[h, c, pair] = bank(n + pair, name)
                 for s in range(2):
                     first = (ROW_TILES * c + 4 * h + 2 * pair + s) * (M // 2)
                     for u in range(2):
@@ -346,14 +349,12 @@ def tile_cauchytransferfunctionfilter_d2p_kernel(
                 in_=f_bf[z][:, c].rearrange("p d t -> p (d t)"),
             )
 
-        def synthesis(z, m):
-            i, first, blocks = PIECES[z]
-            width = P * blocks
-            tiles = 512 // width
-            name = "o%d%d" % (z, m)
-            o_ps = out_bank[z, m] = passing_bank(name) if z < 3 else bank(m, name)
+        def synthesis(z, j0, tiles, held=None):
+            width = P * PIECES[z][2]
+            name = "o%d%d" % (z, j0)
+            o_ps = out_bank[z, j0] = passing_bank(name) if held is None else bank(held, name)
             for s in range(tiles):
-                j = tiles * m + s
+                j = j0 + s
                 for c in range(2):
                     nc.tensor.matmul_mx(
                         out=o_ps[:, cols(s, width)],
@@ -365,23 +366,37 @@ def tile_cauchytransferfunctionfilter_d2p_kernel(
                         stop=(c == 1),
                     )
 
-        def store(z, m, copy=nc.scalar.copy):
+        def store(z, j0, tiles, copy=nc.scalar.copy):
             i, first, blocks = PIECES[z]
             width = P * blocks
-            tiles = 512 // width
-            copy(out=o_sb[z][:, cols(m, tiles), :], in_=out_bank[z, m][:].rearrange("p (j d) -> p j d", d=width))
+            rows = slice(j0, j0 + tiles)
+            copy(
+                out=o_sb[z][:, rows, :],
+                in_=out_bank[z, j0][:, 0 : tiles * width].rearrange("p (j d) -> p j d", d=width),
+            )
             nc.sync.dma_start(
-                out=out[i].rearrange("(p j) d -> p j d", j=ROW_TILES)[
-                    :, cols(m, tiles), P * first : P * first + width
-                ],
-                in_=o_sb[z][:, cols(m, tiles), :],
+                out=out[i].rearrange("(p j) d -> p j d", j=ROW_TILES)[:, rows, P * first : P * first + width],
+                in_=o_sb[z][:, rows, :],
             )
 
-        for tm in range(T):
-            difference(tm, False)
+        def output(z, j0, tiles, held=None, copy=nc.scalar.copy):
+            synthesis(z, j0, tiles, held)
+            store(z, j0, tiles, copy)
+
+        def transfer_kept_for(blk):
+            for c in range(2):
+                transfer(blk, c)
+                keep_transfer(blk, c)
+
+        def f_quantize_parts(z):
+            for c in range(2):
+                f_quantize_part(z, c)
+
+        for tm, n in enumerate((4, 5, 6, 7)):
+            difference(tm, n)
         x_widen(0, 0, cols(1, 2 * D))
         square(0)
-        x_widen(0, 1)
+        x_widen(0, 1, cols(1, 2 * D))
         for tm in range(1, T):
             square(tm)
         inverse_root(0)
@@ -391,8 +406,8 @@ def tile_cauchytransferfunctionfilter_d2p_kernel(
         scales_repeat()
         x_widen(0, 0, cols(0, 2 * D), nc.vector.tensor_copy)
         scales_to_rows()
-        permute_p_codes(0)
-        permute_p_codes(1)
+        permute_p_codes()
+        x_widen(0, 1, cols(0, 2 * D), nc.vector.tensor_copy)
         for g in range(2):
             for h in range(2):
                 x_scale(0, g, h)
@@ -400,72 +415,64 @@ def tile_cauchytransferfunctionfilter_d2p_kernel(
         permute_p_planes()
         weight(0)
         weight(1)
-        q_turn(0, 0)
-        q_turn(0, 1)
-        q_turn(1, 0)
+        q_turn(0, 0, 0)
+        q_turn(0, 1, 2)
+        q_turn(1, 0, 4)
         q_copy(0, 0)
         q_copy(0, 1)
         for tm in range(T):
-            difference(tm, True)
-        q_turn(1, 1)
+            difference(tm, tm)
+        q_turn(1, 1, 6)
         g_real(0)
         g_real(1, nc.gpsimd)
-        for c in range(2):
-            q_copy(1, c)
+        q_copy(1, 0)
+        q_copy(1, 1)
         for tm in range(T):
             g_imaginary(tm)
+        analysis(0, 0)
+        analysis(0, 1)
         x_quantize(0, 1)
         g_quantize(0)
         g_quantize(1)
         q_quantize(0)
-        q_quantize(1)
 
         x_widen(1, 0)
-        analysis(0, 0)
-        analysis(0, 1)
-        for blk in range(BLOCKS):
-            for c in range(2):
-                transfer(blk, c)
-                keep_transfer(blk, c)
-            if blk == 1:
-                x_widen(1, 1)
+        transfer_kept_for(0)
+        transfer_kept_for(1)
         analysis(0, 2)
+        x_widen(1, 1)
+        transfer_kept_for(2)
+        transfer_kept_for(3)
         analysis(0, 3)
-
         filter_block(0, 0)
         filter_block(0, 1)
+        f_quantize_parts(0)
+        q_quantize(1)
         x_scale(1, 0, 0)
-        f_quantize(0)
         x_scale(1, 1, 0)
         x_scale(1, 0, 1, on_scalar=True)
+        for j in range(0, 8, 2):
+            output(0, j, 2)
         x_scale(1, 1, 1, on_scalar=True)
-        for m in range(4):
-            synthesis(0, m)
-            store(0, m)
         filter_part(1, 2, 0)
         x_quantize(1, 0)
         analysis(1, 0)
         analysis(1, 1)
         filter_part(1, 2, 1)
         filter_block(1, 3)
-        x_quantize(1, 1)
-        f_quantize(1)
-        analysis(1, 2)
-        for m in range(4):
-            synthesis(1, m)
-            store(1, m)
-        analysis(1, 3)
+        f_quantize_parts(1)
+        for j in range(0, 8, 2):
+            output(1, j, 2)
         filter_block(2, 0)
+        x_quantize(1, 1)
+        analysis(1, 2)
+        analysis(1, 3)
         filter_block(2, 1)
-        f_quantize_part(2, 0)
-        f_quantize_part(2, 1)
+        f_quantize_parts(2)
         filter_block(3, 2)
         filter_block(3, 3)
-        f_quantize_part(3, 0)
-        f_quantize_part(3, 1)
-        for m in range(4):
-            synthesis(2, m)
-            store(2, m)
-        for m in range(4):
-            synthesis(3, m)
-            store(3, m, nc.vector.tensor_copy if m % 2 == 0 else nc.scalar.copy)
+        f_quantize_parts(3)
+        for j, n in enumerate((4, 0, 1, 5, 6, 7, 4, 0)):
+            output(2, j, 1, held=n)
+        for j, n in enumerate((1, 2, 3, 5, 6, 7, 4, 0)):
+            output(3, j, 1, held=n, copy=nc.vector.tensor_copy if j % 2 == 0 else nc.scalar.copy)

@@ -20,6 +20,7 @@ B, S, D, M, N = 2, 1024, 512, 512, 512
 P = 128
 T = 4
 RUN = 4
+LINE = 8
 BLOCKS = D // P
 ROW_TILES = S // P
 
@@ -82,7 +83,8 @@ def tile_cauchytransferfunctionfilter_d2p_kernel(
 
         x_raw = [[sb("x_raw%d%d" % (i, g), [P, T, D], U8) for g in range(2)] for i in range(B)]
         x_wide = [[sb("x_wide%d%d" % (i, g), [P, T, D], BF16) for g in range(2)] for i in range(B)]
-        x_bf = [[sb("x_bf%d%d" % (i, h), [P, 2, 2 * P, T], BF16) for h in range(2)] for i in range(B)]
+        x_bf = {(i, h): sb("x_bf%d%d" % (i, h), [P, 2, 2 * P, T], BF16) for i, h in ((0, 0), (0, 1))}
+        x_last = {}
         x_codes = [[sb("x_codes%d%d" % (i, h), [P, 2, 2 * P], U32) for h in range(2)] for i in range(B)]
         x_planes = [[sb("x_planes%d%d" % (i, h), [P, 2, 2 * P], U8) for h in range(2)] for i in range(B)]
         xs_rows = sb("xs_rows", [P, 32], F32)
@@ -133,8 +135,8 @@ def tile_cauchytransferfunctionfilter_d2p_kernel(
         )
         nc.scalar.activation(out=warm_out[:], in_=warm_in[:], func=ACT.Abs_reciprocal_sqrt)
         load_x(0, 0)
-        nc.sync.dma_start(out=p_raw[:].bitcast(I32), in_=p_words.rearrange("g p n -> p g n").bitcast(I32))
         load_x(0, 1)
+        nc.sync.dma_start(out=p_raw[:].bitcast(I32), in_=p_words.rearrange("g p n -> p g n").bitcast(I32))
         nc.sync.dma_start(out=b_col[:], in_=b.rearrange("(p t) -> p t", t=T))
         load_q(0, 0)
         load_q(0, 1)
@@ -235,8 +237,8 @@ def tile_cauchytransferfunctionfilter_d2p_kernel(
 
         def permute_p_codes():
             nc.vector.tensor_copy(
-                out=p_codes[:].bitcast(U16).rearrange("p g (t n) -> p g t n", t=T),
-                in_=p_raw[:].bitcast(U16).rearrange("p g (n t) -> p g t n", t=T),
+                out=p_codes[:].bitcast(U16).rearrange("p g (t r i) -> p g r t i", t=T, i=LINE),
+                in_=p_raw[:].bitcast(U16).rearrange("p g (r i t) -> p g r t i", t=T, i=LINE),
             )
 
         def permute_p_planes():
@@ -254,29 +256,54 @@ def tile_cauchytransferfunctionfilter_d2p_kernel(
         def scales_to_rows():
             nc.vector.transpose(out=x_s[:], in_=xs_spread[:])
 
-        def x_widen(i, g, part=slice(0, T * D), copy=nc.scalar.copy):
-            copy(
-                out=x_wide[i][g][:].rearrange("p t d -> p (t d)")[:, part],
-                in_=x_raw[i][g][:].rearrange("p t d -> p (t d)")[:, part].bitcast(FP8),
-            )
+        def x_widen(i, g, part=slice(0, T * D), on_vector=False):
+            wide = x_wide[i][g][:].rearrange("p t d -> p (t d)")[:, part]
+            raw = x_raw[i][g][:].rearrange("p t d -> p (t d)")[:, part].bitcast(FP8)
+            if on_vector:
+                nc.vector.tensor_scalar(out=wide, in0=raw, scalar1=1.0, scalar2=None, op0=MULT)
+            else:
+                nc.scalar.copy(out=wide, in_=raw)
 
-        def x_scale(i, g, h, on_scalar=False):
-            for blk in (2 * h, 2 * h + 1):
-                column = BLOCKS * (2 * i + g) + blk
-                scale = x_s[:, column : column + 1]
-                words = runs_of_words(x_bf[i][h][:, g, cols(blk % 2), :])
-                values = x_wide[i][g][:, :, cols(blk)].rearrange("p t (g i) -> p g t i", i=RUN)
-                if on_scalar:
-                    nc.scalar.activation(out=words, in_=values, func=ACT.Copy, scale=scale)
-                else:
-                    nc.vector.tensor_scalar(out=words, in0=values, scalar1=scale, scalar2=None, op0=MULT)
+        def scale_block(i, g, blk, words, engine):
+            column = BLOCKS * (2 * i + g) + blk
+            scale = x_s[:, column : column + 1]
+            values = x_wide[i][g][:, :, cols(blk)]
+            runs = values.rearrange("p t (g i) -> p g t i", i=RUN)
+            if engine == "scalar":
+                nc.scalar.activation(out=runs_of_words(words), in_=runs, func=ACT.Copy, scale=scale)
+            elif engine == "vector":
+                nc.vector.tensor_scalar(out=runs_of_words(words), in0=runs, scalar1=scale, scalar2=None, op0=MULT)
+            else:
+                nc.gpsimd.tensor_scalar(
+                    out=words, in0=values.rearrange("p t d -> p d t"), scalar1=scale, scalar2=0.0, op0=MULT, op1=ADD
+                )
+
+        def x_scale(i, g, blk, engine="vector"):
+            scale_block(i, g, blk, x_bf[i, blk // 2][:, g, cols(blk % 2), :], engine)
 
         def x_quantize(i, h):
             nc.vector.quantize_mx(
                 out=x_codes[i][h][:].rearrange("p g d -> p (g d)").bitcast(E4M3),
                 scales=x_planes[i][h][:].rearrange("p g d -> p (g d)"),
-                in_=x_bf[i][h][:].rearrange("p g d t -> p (g d t)"),
+                in_=x_bf[i, h][:].rearrange("p g d t -> p (g d t)"),
             )
+
+        def taken_over(name, shape):
+            return keep.tile(shape, BF16, name=name, tag="q_bf0", align_bytes=64)
+
+        def x_last_scale(g, blk, engine):
+            name = "x_last%d%d" % (g, blk)
+            make = taken_over if engine == "gpsimd" else lambda name, shape: sb(name, shape, BF16)
+            x_last[g, blk] = make(name, [P, P, T])
+            scale_block(1, g, blk, x_last[g, blk][:], engine)
+
+        def x_last_quantize(blk):
+            for g in range(2):
+                nc.vector.quantize_mx(
+                    out=x_codes[1][1][:, g, cols(blk % 2)].bitcast(E4M3),
+                    scales=x_planes[1][1][:, g, cols(blk % 2)],
+                    in_=x_last[g, blk][:].rearrange("p d t -> p (d t)"),
+                )
 
         def analysis(i, blk):
             u_ps = u_bank[i, blk] = bank(blk, "u%d%d" % (i, blk))
@@ -366,22 +393,31 @@ def tile_cauchytransferfunctionfilter_d2p_kernel(
                         stop=(c == 1),
                     )
 
-        def store(z, j0, tiles, copy=nc.scalar.copy):
-            i, first, blocks = PIECES[z]
-            width = P * blocks
-            rows = slice(j0, j0 + tiles)
+        def copy_out(z, j0, tiles, copy):
+            width = P * PIECES[z][2]
             copy(
-                out=o_sb[z][:, rows, :],
+                out=o_sb[z][:, j0 : j0 + tiles, :],
                 in_=out_bank[z, j0][:, 0 : tiles * width].rearrange("p (j d) -> p j d", d=width),
             )
+
+        def store(z, j0, tiles):
+            i, first, blocks = PIECES[z]
+            rows = slice(j0, j0 + tiles)
             nc.sync.dma_start(
-                out=out[i].rearrange("(p j) d -> p j d", j=ROW_TILES)[:, rows, P * first : P * first + width],
+                out=out[i].rearrange("(p j) d -> p j d", j=ROW_TILES)[:, rows, P * first : P * (first + blocks)],
                 in_=o_sb[z][:, rows, :],
             )
 
         def output(z, j0, tiles, held=None, copy=nc.scalar.copy):
             synthesis(z, j0, tiles, held)
-            store(z, j0, tiles, copy)
+            copy_out(z, j0, tiles, copy)
+            store(z, j0, tiles)
+
+        def output_half(z, h):
+            for j0 in (4 * h, 4 * h + 2):
+                synthesis(z, j0, 2)
+                copy_out(z, j0, 2, nc.scalar.copy)
+            store(z, 4 * h, 4)
 
         def transfer_kept_for(blk):
             for c in range(2):
@@ -404,13 +440,13 @@ def tile_cauchytransferfunctionfilter_d2p_kernel(
 
         scales_to_columns()
         scales_repeat()
-        x_widen(0, 0, cols(0, 2 * D), nc.vector.tensor_copy)
+        x_widen(0, 0, cols(0, 2 * D), on_vector=True)
         scales_to_rows()
+        x_widen(0, 1, cols(0, 2 * D), on_vector=True)
         permute_p_codes()
-        x_widen(0, 1, cols(0, 2 * D), nc.vector.tensor_copy)
         for g in range(2):
-            for h in range(2):
-                x_scale(0, g, h)
+            for blk in range(BLOCKS):
+                x_scale(0, g, blk)
         x_quantize(0, 0)
         permute_p_planes()
         weight(0)
@@ -437,42 +473,59 @@ def tile_cauchytransferfunctionfilter_d2p_kernel(
         q_quantize(0)
 
         x_widen(1, 0)
+        x_bf[1, 0] = taken_over("x_bf10", [P, 2, 2 * P, T])
+        x_scale(1, 0, 0, "gpsimd")
         transfer_kept_for(0)
         transfer_kept_for(1)
         analysis(0, 2)
         x_widen(1, 1)
-        transfer_kept_for(2)
-        transfer_kept_for(3)
+        transfer(2, 0)
+        keep_transfer(2, 0)
+        x_scale(1, 1, 0, "scalar")
+        x_scale(1, 1, 1, "scalar")
+        transfer(2, 1)
+        keep_transfer(2, 1)
         analysis(0, 3)
         filter_block(0, 0)
         filter_block(0, 1)
         f_quantize_parts(0)
         q_quantize(1)
-        x_scale(1, 0, 0)
-        x_scale(1, 1, 0)
-        x_scale(1, 0, 1, on_scalar=True)
-        for j in range(0, 8, 2):
-            output(0, j, 2)
-        x_scale(1, 1, 1, on_scalar=True)
+        x_scale(1, 0, 1)
+        synthesis(0, 0, 2, 0)
+        transfer(3, 0)
+        keep_transfer(3, 0)
+        copy_out(0, 0, 2, nc.scalar.copy)
+        store(0, 0, 2)
+        transfer(3, 1)
+        keep_transfer(3, 1)
+        output(0, 2, 2, held=1)
+        x_last_scale(0, 2, "scalar")
+        output(0, 4, 2)
+        output(0, 6, 2)
+        x_last_scale(0, 3, "scalar")
         filter_part(1, 2, 0)
         x_quantize(1, 0)
+        x_last_scale(1, 2, "gpsimd")
         analysis(1, 0)
         analysis(1, 1)
         filter_part(1, 2, 1)
         filter_block(1, 3)
         f_quantize_parts(1)
+        x_last_quantize(2)
+        x_last_scale(1, 3, "gpsimd")
         for j in range(0, 8, 2):
             output(1, j, 2)
-        filter_block(2, 0)
-        x_quantize(1, 1)
         analysis(1, 2)
+        filter_block(2, 0)
+        filter_part(2, 1, 0)
+        x_last_quantize(3)
         analysis(1, 3)
-        filter_block(2, 1)
+        filter_part(2, 1, 1)
         f_quantize_parts(2)
         filter_block(3, 2)
         filter_block(3, 3)
         f_quantize_parts(3)
-        for j, n in enumerate((4, 0, 1, 5, 6, 7, 4, 0)):
-            output(2, j, 1, held=n)
-        for j, n in enumerate((1, 2, 3, 5, 6, 7, 4, 0)):
-            output(3, j, 1, held=n, copy=nc.vector.tensor_copy if j % 2 == 0 else nc.scalar.copy)
+        for j in range(0, 8, 2):
+            output(2, j, 2)
+        for m in range(4):
+            output(3, 2 * m, 2, held=m, copy=nc.vector.tensor_copy if m % 2 == 0 else nc.scalar.copy)

@@ -332,9 +332,9 @@ def tile_cauchytransferfunctionfilter_d2p_kernel(
                             turned[:, cols(2 * s + u)], q_pairs[:, first + u : first + M // 2 : 2], identity[:]
                         )
 
-        def q_copy(h, c):
-            for pair in range(2):
-                nc.scalar.copy(
+        def q_copy(h, c, pairs=range(2), copy=nc.scalar.copy):
+            for pair in pairs:
+                copy(
                     out=q_bf[h][:, c, cols(pair, 2)]
                     .rearrange("p s r e -> p (s r e)")
                     .bitcast(F32)
@@ -443,10 +443,11 @@ def tile_cauchytransferfunctionfilter_d2p_kernel(
         x_widen(0, 0, cols(0, 2 * D), on_vector=True)
         scales_to_rows()
         x_widen(0, 1, cols(0, 2 * D), on_vector=True)
+        for blk in range(BLOCKS):
+            x_scale(0, 0, blk)
         permute_p_codes()
-        for g in range(2):
-            for blk in range(BLOCKS):
-                x_scale(0, g, blk)
+        for blk in range(BLOCKS):
+            x_scale(0, 1, blk)
         x_quantize(0, 0)
         permute_p_planes()
         weight(0)
@@ -462,9 +463,11 @@ def tile_cauchytransferfunctionfilter_d2p_kernel(
         g_real(0)
         g_real(1, nc.gpsimd)
         q_copy(1, 0)
-        q_copy(1, 1)
+        x_widen(1, 0)
+        q_copy(1, 1, [1])
         for tm in range(T):
             g_imaginary(tm)
+        q_copy(1, 1, [0], nc.vector.tensor_copy)
         analysis(0, 0)
         analysis(0, 1)
         x_quantize(0, 1)
@@ -472,13 +475,12 @@ def tile_cauchytransferfunctionfilter_d2p_kernel(
         g_quantize(1)
         q_quantize(0)
 
-        x_widen(1, 0)
         x_bf[1, 0] = taken_over("x_bf10", [P, 2, 2 * P, T])
         x_scale(1, 0, 0, "gpsimd")
+        x_widen(1, 1)
         transfer_kept_for(0)
         transfer_kept_for(1)
         analysis(0, 2)
-        x_widen(1, 1)
         transfer(2, 0)
         keep_transfer(2, 0)
         x_scale(1, 1, 0, "scalar")
@@ -486,33 +488,30 @@ def tile_cauchytransferfunctionfilter_d2p_kernel(
         transfer(2, 1)
         keep_transfer(2, 1)
         analysis(0, 3)
+        transfer(3, 0)
+        transfer(3, 1)
         filter_block(0, 0)
         filter_block(0, 1)
         f_quantize_parts(0)
-        q_quantize(1)
         x_scale(1, 0, 1)
-        synthesis(0, 0, 2, 0)
-        transfer(3, 0)
+        q_quantize(1)
+        x_quantize(1, 0)
+        x_last_scale(1, 2, "gpsimd")
         keep_transfer(3, 0)
-        copy_out(0, 0, 2, nc.scalar.copy)
-        store(0, 0, 2)
-        transfer(3, 1)
+        output(0, 0, 2, held=0)
         keep_transfer(3, 1)
         output(0, 2, 2, held=1)
         x_last_scale(0, 2, "scalar")
         output(0, 4, 2)
         output(0, 6, 2)
         x_last_scale(0, 3, "scalar")
-        filter_part(1, 2, 0)
-        x_quantize(1, 0)
-        x_last_scale(1, 2, "gpsimd")
+        x_last_scale(1, 3, "scalar")
         analysis(1, 0)
         analysis(1, 1)
-        filter_part(1, 2, 1)
+        filter_block(1, 2)
         filter_block(1, 3)
         f_quantize_parts(1)
         x_last_quantize(2)
-        x_last_scale(1, 3, "gpsimd")
         for j in range(0, 8, 2):
             output(1, j, 2)
         analysis(1, 2)

@@ -82,15 +82,12 @@ def tile_cauchytransferfunctionfilter_d2p_kernel(
         p_planes = sb("p_planes", [P, 2, M], U8)
 
         x_raw = [[sb("x_raw%d%d" % (i, g), [P, T, D], U8) for g in range(2)] for i in range(B)]
-        x_wide = [[sb("x_wide%d%d" % (i, g), [P, T, D], BF16) for g in range(2)] for i in range(B)]
+        x_wide = [sb("x_wide%d" % g, [P, T, D], BF16) for g in range(2)]
         x_bf = {(i, h): sb("x_bf%d%d" % (i, h), [P, 2, 2 * P, T], BF16) for i, h in ((0, 0), (0, 1))}
         x_last = {}
         x_codes = [[sb("x_codes%d%d" % (i, h), [P, 2, 2 * P], U32) for h in range(2)] for i in range(B)]
         x_planes = [[sb("x_planes%d%d" % (i, h), [P, 2, 2 * P], U8) for h in range(2)] for i in range(B)]
-        xs_rows = sb("xs_rows", [P, 32], F32)
-        xs_columns = sb("xs_columns", [P, 32], F32)
-        xs_spread = sb("xs_spread", [P, 32], F32)
-        x_s = sb("x_s", [P, 32], F32)
+        x_s = sb("x_s", [P, 2 * B, 2 * BLOCKS], F32)
 
         identity = sb("identity", [P, P], F32)
         q_raw = sb("q_raw", [P, 2, ROW_TILES, M], BF16)
@@ -105,7 +102,6 @@ def tile_cauchytransferfunctionfilter_d2p_kernel(
 
         difference_bank, transfer_bank, q_bank, u_bank, out_bank = {}, {}, {}, {}, {}
 
-        nc.vector.memset(xs_rows[:], 0.0)
         warm_in = sb("warm_in", [P, 1], F32)
         warm_out = sb("warm_out", [P, 1], F32)
         nc.vector.memset(warm_in[:], 1.0)
@@ -129,10 +125,11 @@ def tile_cauchytransferfunctionfilter_d2p_kernel(
 
         nc.sync.dma_start(out=right[127:128, :], in_=om.rearrange("(o m) -> o m", o=1))
         nc.sync.dma_start(out=left[63:64, :], in_=nu.rearrange("(o n) -> o n", o=1))
-        nc.sync.dma_start(
-            out=xs_rows[0:128:32, 0:16].rearrange("a (n j) -> a n j", j=BLOCKS),
-            in_=x_scale.rearrange("i (g a) j -> a (i g) j", a=4),
-        )
+        for quad in range(4):
+            nc.sync.dma_start(
+                out=x_s[cols(quad, 32), :, 0:BLOCKS],
+                in_=x_scale.rearrange("i (g a) j -> a (i g) j", a=4)[quad].partition_broadcast(32),
+            )
         nc.scalar.activation(out=warm_out[:], in_=warm_in[:], func=ACT.Abs_reciprocal_sqrt)
         load_x(0, 0)
         load_x(0, 1)
@@ -247,27 +244,15 @@ def tile_cauchytransferfunctionfilter_d2p_kernel(
                 in_=p_raw_planes[:].rearrange("p g (n t) -> p g t n", t=T),
             )
 
-        def scales_to_columns():
-            nc.vector.transpose(out=xs_columns[:], in_=xs_rows[:])
-
-        def scales_repeat():
-            nc.vector.tensor_copy(out=xs_spread[:], in_=xs_columns[:, 0:1].to_broadcast([P, 32]))
-
-        def scales_to_rows():
-            nc.vector.transpose(out=x_s[:], in_=xs_spread[:])
-
-        def x_widen(i, g, part=slice(0, T * D), on_vector=False):
-            wide = x_wide[i][g][:].rearrange("p t d -> p (t d)")[:, part]
-            raw = x_raw[i][g][:].rearrange("p t d -> p (t d)")[:, part].bitcast(FP8)
-            if on_vector:
-                nc.vector.tensor_scalar(out=wide, in0=raw, scalar1=1.0, scalar2=None, op0=MULT)
-            else:
-                nc.scalar.copy(out=wide, in_=raw)
+        def x_widen(i, g):
+            nc.scalar.copy(
+                out=x_wide[g][:].rearrange("p t d -> p (t d)"),
+                in_=x_raw[i][g][:].rearrange("p t d -> p (t d)").bitcast(FP8),
+            )
 
         def scale_block(i, g, blk, words, engine):
-            column = BLOCKS * (2 * i + g) + blk
-            scale = x_s[:, column : column + 1]
-            values = x_wide[i][g][:, :, cols(blk)]
+            scale = x_s[:, 2 * i + g, blk : blk + 1]
+            values = (x_raw[i][g][:].bitcast(FP8) if engine == "vector" else x_wide[g][:])[:, :, cols(blk)]
             runs = values.rearrange("p t (g i) -> p g t i", i=RUN)
             if engine == "scalar":
                 nc.scalar.activation(out=runs_of_words(words), in_=runs, func=ACT.Copy, scale=scale)
@@ -430,19 +415,11 @@ def tile_cauchytransferfunctionfilter_d2p_kernel(
 
         for tm, n in enumerate((4, 5, 6, 7)):
             difference(tm, n)
-        x_widen(0, 0, cols(1, 2 * D))
-        square(0)
-        x_widen(0, 1, cols(1, 2 * D))
-        for tm in range(1, T):
+        for tm in range(T):
             square(tm)
         inverse_root(0)
         inverse_root(1)
 
-        scales_to_columns()
-        scales_repeat()
-        x_widen(0, 0, cols(0, 2 * D), on_vector=True)
-        scales_to_rows()
-        x_widen(0, 1, cols(0, 2 * D), on_vector=True)
         for blk in range(BLOCKS):
             x_scale(0, 0, blk)
         permute_p_codes()

@@ -87,7 +87,10 @@ def tile_cauchytransferfunctionfilter_d2p_kernel(
         x_last = {}
         x_codes = [[sb("x_codes%d%d" % (i, h), [P, 2, 2 * P], U32) for h in range(2)] for i in range(B)]
         x_planes = [[sb("x_planes%d%d" % (i, h), [P, 2, 2 * P], U8) for h in range(2)] for i in range(B)]
-        x_s = sb("x_s", [P, 2 * B, 2 * BLOCKS], F32)
+        xs_rows = sb("xs_rows", [P, 32], F32)
+        xs_columns = sb("xs_columns", [P, 32], F32)
+        xs_spread = sb("xs_spread", [P, 32], F32)
+        x_s = sb("x_s", [P, 32], F32)
 
         identity = sb("identity", [P, P], F32)
         q_raw = sb("q_raw", [P, 2, ROW_TILES, M], BF16)
@@ -102,6 +105,7 @@ def tile_cauchytransferfunctionfilter_d2p_kernel(
 
         difference_bank, transfer_bank, q_bank, u_bank, out_bank = {}, {}, {}, {}, {}
 
+        nc.vector.memset(xs_rows[:], 0.0)
         warm_in = sb("warm_in", [P, 1], F32)
         warm_out = sb("warm_out", [P, 1], F32)
         nc.vector.memset(warm_in[:], 1.0)
@@ -125,11 +129,10 @@ def tile_cauchytransferfunctionfilter_d2p_kernel(
 
         nc.sync.dma_start(out=right[127:128, :], in_=om.rearrange("(o m) -> o m", o=1))
         nc.sync.dma_start(out=left[63:64, :], in_=nu.rearrange("(o n) -> o n", o=1))
-        for quad in range(4):
-            nc.sync.dma_start(
-                out=x_s[cols(quad, 32), :, 0:BLOCKS],
-                in_=x_scale.rearrange("i (g a) j -> a (i g) j", a=4)[quad].partition_broadcast(32),
-            )
+        nc.sync.dma_start(
+            out=xs_rows[0:128:32, 0:16].rearrange("a (n j) -> a n j", j=BLOCKS),
+            in_=x_scale.rearrange("i (g a) j -> a (i g) j", a=4),
+        )
         nc.scalar.activation(out=warm_out[:], in_=warm_in[:], func=ACT.Abs_reciprocal_sqrt)
         load_x(0, 0)
         load_x(0, 1)
@@ -244,6 +247,15 @@ def tile_cauchytransferfunctionfilter_d2p_kernel(
                 in_=p_raw_planes[:].rearrange("p g (n t) -> p g t n", t=T),
             )
 
+        def scales_to_columns():
+            nc.vector.transpose(out=xs_columns[:], in_=xs_rows[:])
+
+        def scales_repeat():
+            nc.vector.tensor_copy(out=xs_spread[:], in_=xs_columns[:, 0:1].to_broadcast([P, 32]))
+
+        def scales_to_rows():
+            nc.vector.transpose(out=x_s[:], in_=xs_spread[:])
+
         def x_widen(i, g):
             nc.scalar.copy(
                 out=x_wide[g][:].rearrange("p t d -> p (t d)"),
@@ -251,7 +263,8 @@ def tile_cauchytransferfunctionfilter_d2p_kernel(
             )
 
         def scale_block(i, g, blk, words, engine):
-            scale = x_s[:, 2 * i + g, blk : blk + 1]
+            column = BLOCKS * (2 * i + g) + blk
+            scale = x_s[:, column : column + 1]
             values = (x_raw[i][g][:].bitcast(FP8) if engine == "vector" else x_wide[g][:])[:, :, cols(blk)]
             runs = values.rearrange("p t (g i) -> p g t i", i=RUN)
             if engine == "scalar":
@@ -420,6 +433,9 @@ def tile_cauchytransferfunctionfilter_d2p_kernel(
         inverse_root(0)
         inverse_root(1)
 
+        scales_to_columns()
+        scales_repeat()
+        scales_to_rows()
         for blk in range(BLOCKS):
             x_scale(0, 0, blk)
         permute_p_codes()

@@ -64,7 +64,8 @@ def tile_cauchytransferfunctionfilter_d2p_kernel(
 
         left = sb("left", [P, N], BF16)
         right = sb("right", [P, M], BF16)
-        b_col = sb("b_col", [P, T], BF16)
+        first_rows = sb("first_rows", [P, 1], BF16)
+        b_col = sb("b_col", [P, T], F32)
         squares = sb("squares", [P, T, M], F32)
         roots = sb("roots", [P, T, M], F32)
         w = sb("w", [P, T, M], F32)
@@ -109,10 +110,14 @@ def tile_cauchytransferfunctionfilter_d2p_kernel(
         warm_in = sb("warm_in", [P, 1], F32)
         warm_out = sb("warm_out", [P, 1], F32)
         nc.vector.memset(warm_in[:], 1.0)
+        nc.vector.memset(left[0:31, :], 0.0)
+        nc.vector.memset(left[32:63, :], 0.0)
         nc.vector.memset(left[64:128, :], 1.0)
-        nc.vector.memset(right[0:127, :], -1.0)
-        nc.vector.memset(left[0:63, :], 0.0)
-        nc.vector.memset(left[64:127, :], 0.0)
+        nc.vector.memset(right[0:32, :], 0.0)
+        nc.vector.memset(right[32:64, :], -1.0)
+        nc.vector.memset(right[64:127, :], 0.0)
+        nc.vector.memset(first_rows[:], 0.0)
+        nc.vector.memset(first_rows[0:32, :], 1.0)
         nc.vector.memset(p_raw_planes[:].rearrange("p g n -> p (g n)").bitcast(I32), 0)
         nc.vector.memset(c_planes[:].bitcast(I32), 0)
 
@@ -129,6 +134,7 @@ def tile_cauchytransferfunctionfilter_d2p_kernel(
 
         nc.sync.dma_start(out=right[127:128, :], in_=om.rearrange("(o m) -> o m", o=1))
         nc.sync.dma_start(out=left[63:64, :], in_=nu.rearrange("(o n) -> o n", o=1))
+        nc.sync.dma_start(out=left[31:32, :], in_=b.rearrange("(o n) -> o n", o=1))
         nc.sync.dma_start(
             out=xs_rows[0:128:32, 0:16].rearrange("a (n j) -> a n j", j=BLOCKS),
             in_=x_scale.rearrange("i (g a) j -> a (i g) j", a=4),
@@ -137,7 +143,6 @@ def tile_cauchytransferfunctionfilter_d2p_kernel(
         load_x(0, 0)
         load_x(0, 1)
         nc.sync.dma_start(out=p_raw[:].bitcast(I32), in_=p_words.rearrange("g p n -> p g n").bitcast(I32))
-        nc.sync.dma_start(out=b_col[:], in_=b.rearrange("(p t) -> p t", t=T))
         load_q(0, 0)
         load_q(0, 1)
         for quad in range(4):
@@ -161,6 +166,12 @@ def tile_cauchytransferfunctionfilter_d2p_kernel(
             d = difference_bank[tm] = bank(n, "difference%d%d" % (tm, n))
             for t in range(T):
                 nc.tensor.matmul(d[:, cols(t)], lhsT=left[:, t::T], rhs=right[:, tm::T], start=True, stop=True)
+
+        def spread_b(n):
+            b_ps = bank(n, "b_ps")
+            for t in range(T):
+                nc.tensor.matmul(b_ps[:, t : t + 1], lhsT=left[:, t::T], rhs=first_rows[:], start=True, stop=True)
+            return b_ps
 
         def square(tm):
             nc.scalar.activation(
@@ -428,6 +439,7 @@ def tile_cauchytransferfunctionfilter_d2p_kernel(
 
         for tm, n in enumerate((4, 5, 6, 7)):
             difference(tm, n)
+        b_ps = spread_b(0)
         for tm in range(T):
             square(tm)
         inverse_root(0)
@@ -439,6 +451,7 @@ def tile_cauchytransferfunctionfilter_d2p_kernel(
         for blk in range(BLOCKS):
             x_scale(0, 0, blk)
         permute_p_codes()
+        nc.vector.tensor_copy(out=b_col[:], in_=b_ps[:, 0:T])
         for blk in range(BLOCKS):
             x_scale(0, 1, blk)
         x_quantize(0, 0)

@@ -23,10 +23,15 @@ RUN = 4
 LINE = 8
 BLOCKS = D // P
 ROW_TILES = S // P
+ONES = 0x3F803F80
+MINUS_ONES = 0xBF80BF80
 
 FLOPS = 2 * (2 * M * N * D + B * M * S * D + 2 * B * S * M * D)
 
+
 PIECES = ((0, 0, 2), (0, 2, 2), (1, 0, 2), (1, 2, 2))
+ON_GPSIMD = ((1, 0, 0), (1, 1, 2))
+APART = tuple((i, g, blk) for i, h, blk in ON_GPSIMD for g in range(2))
 
 
 def tile_cauchytransferfunctionfilter_d2p_kernel(
@@ -41,37 +46,39 @@ def tile_cauchytransferfunctionfilter_d2p_kernel(
         def bank(n, name):
             return psum.tile([P, 512], F32, tag="bank%d" % n, name=name)
 
-        passed = []
-
-        def passing_bank(name):
-            passed.append(name)
-            return bank(4 + (len(passed) - 1) % 4, name)
-
-        def sb(name, shape, dt):
-            return keep.tile(shape, dt, name=name, align_bytes=64)
+        def sb(name, shape, dt, tag=None):
+            return keep.tile(shape, dt, name=name, tag=tag or name, align_bytes=64)
 
         def cols(n, width=P):
             return slice(width * n, width * n + width)
 
-        def by_runs(ap):
-            return ap.rearrange("p (t g i) -> p g t i", t=T, i=RUN)
+        def by_runs(ap, run=RUN):
+            return ap.rearrange("p t (g i) -> p g t i", i=run)
+
+        def slices(ap):
+            return ap.rearrange("p (t d) -> p t d", t=T)
 
         def by_words(ap):
             return ap.rearrange("p (t d) -> p d t", t=T)
 
-        def runs_of_words(ap):
-            return ap.rearrange("p (g i) t -> p g t i", i=RUN)
+        def runs_of_words(ap, run=RUN):
+            return ap.rearrange("p (g i) t -> p g t i", i=run)
+
+        def quantize(codes, planes, values):
+            nc.vector.quantize_mx(out=codes.bitcast(E4M3), scales=planes, in_=values)
 
         left = sb("left", [P, N], BF16)
         right = sb("right", [P, M], BF16)
-        first_rows = sb("first_rows", [P, 1], BF16)
+        b_rows = sb("b_rows", [P, N], BF16)
+        ones = sb("ones", [P, 1], BF16)
         b_col = sb("b_col", [P, T], F32)
         squares = sb("squares", [P, T, M], F32)
         roots = sb("roots", [P, T, M], F32)
+        inverses = sb("inverses", [P, T, M], F32)
         w = sb("w", [P, T, M], F32)
         g_bf = [sb("g_bf%d" % c, [P, M, T], BF16) for c in range(2)]
         g_codes = [sb("g_codes%d" % c, [P, M], U32) for c in range(2)]
-        g_scales = [sb("g_scales%d" % c, [P, M], U8) for c in range(2)]
+        g_planes = [sb("g_planes%d" % c, [P, M], U8) for c in range(2)]
 
         c_codes = sb("c_codes", [P, 2 * D], U8)
         c_planes = sb("c_planes", [P, D], U8)
@@ -82,12 +89,19 @@ def tile_cauchytransferfunctionfilter_d2p_kernel(
         p_codes = sb("p_codes", [P, 2, 2 * M], U8)
         p_planes = sb("p_planes", [P, 2, M], U8)
 
-        x_raw = [[sb("x_raw%d%d" % (i, g), [P, T, D], U8) for g in range(2)] for i in range(B)]
-        x_wide = [sb("x_wide%d" % g, [P, T, D], BF16) for g in range(2)]
-        x_bf = {(i, h): sb("x_bf%d%d" % (i, h), [P, 2, 2 * P, T], BF16) for i, h in ((0, 0), (0, 1))}
-        x_last = {}
-        x_codes = [[sb("x_codes%d%d" % (i, h), [P, 2, 2 * P], U32) for h in range(2)] for i in range(B)]
-        x_planes = [[sb("x_planes%d%d" % (i, h), [P, 2, 2 * P], U8) for h in range(2)] for i in range(B)]
+        x_raw = [sb("x_raw%d" % i, [P, 2, T, D], U8) for i in range(B)]
+        x_bf = {
+            (i, g, blk): sb("x_bf%d%d%d" % (i, g, blk), [P, P, T], BF16)[:] for i, g, blk in APART if (i, g, blk) not in ON_GPSIMD
+        }
+        x_both = {}
+        for i in range(B):
+            for blk in range(BLOCKS):
+                if (i, 0, blk) not in APART:
+                    x_both[i, blk] = sb("x_both%d%d" % (i, blk), [P, 2, P, T], BF16)
+                    for g in range(2):
+                        x_bf[i, g, blk] = x_both[i, blk][:, g]
+        x_codes = {(i, blk): sb("x_codes%d%d" % (i, blk), [P, 2, P], U32) for i in range(B) for blk in range(BLOCKS)}
+        x_planes = {ib: sb("x_planes%d%d" % ib, [P, 2, P], U8) for ib in x_codes}
         xs_rows = sb("xs_rows", [P, 32], F32)
         xs_columns = sb("xs_columns", [P, 32], F32)
         xs_spread = sb("xs_spread", [P, 32], F32)
@@ -95,71 +109,76 @@ def tile_cauchytransferfunctionfilter_d2p_kernel(
 
         identity = sb("identity", [P, P], F32)
         q_raw = sb("q_raw", [P, 2, ROW_TILES, M], BF16)
-        q_bf = [sb("q_bf%d" % h, [P, 2, 4, P, T], BF16) for h in range(2)]
-        q_codes = [sb("q_codes%d" % h, [P, 2, 4 * P], U32) for h in range(2)]
-        q_planes = [sb("q_planes%d" % h, [P, 2, 4 * P], U8) for h in range(2)]
+        q_bf = {(h, c): sb("q_bf%d%d" % (h, c), [P, 4, P, T], BF16) for h in range(2) for c in range(2)}
+        q_codes = {hc: sb("q_codes%d%d" % hc, [P, 4 * P], U32) for hc in q_bf}
+        q_planes = {hc: sb("q_planes%d%d" % hc, [P, 4 * P], U8) for hc in q_bf}
 
-        f_bf = [sb("f_bf%d" % z, [P, 2, P * PIECES[z][2], T], BF16) for z in range(len(PIECES))]
+        f_bf = {(z, c): sb("f_bf%d%d" % (z, c), [P, PIECES[z][2], P, T], BF16) for z in range(len(PIECES)) for c in range(2)}
         f_codes = [sb("f_codes%d" % z, [P, 2, P * PIECES[z][2]], U32) for z in range(len(PIECES))]
         f_planes = [sb("f_planes%d" % z, [P, 2, P * PIECES[z][2]], U8) for z in range(len(PIECES))]
         o_sb = [sb("o_sb%d" % z, [P, ROW_TILES, P * PIECES[z][2]], F32) for z in range(len(PIECES))]
+        x_wide, u_kept, f_apart = {}, {}, {}
 
         difference_bank, transfer_bank, q_bank, u_bank, out_bank = {}, {}, {}, {}, {}
 
         nc.vector.memset(xs_rows[:], 0.0)
+        nc.vector.memset(p_raw_planes[:].rearrange("p g n -> p (g n)").bitcast(I32), 0)
         warm_in = sb("warm_in", [P, 1], F32)
         warm_out = sb("warm_out", [P, 1], F32)
         nc.vector.memset(warm_in[:], 1.0)
-        nc.vector.memset(left[0:31, :], 0.0)
-        nc.vector.memset(left[32:63, :], 0.0)
-        nc.vector.memset(left[64:128, :], 1.0)
-        nc.vector.memset(right[0:32, :], 0.0)
-        nc.vector.memset(right[32:64, :], -1.0)
+        nc.vector.memset(left[0:63, :], 0.0)
+        nc.vector.memset(left[64:128, :].bitcast(U32), ONES)
+        nc.vector.memset(right[0:64, :].bitcast(U32), MINUS_ONES)
         nc.vector.memset(right[64:127, :], 0.0)
-        nc.vector.memset(first_rows[:], 0.0)
-        nc.vector.memset(first_rows[0:32, :], 1.0)
-        nc.vector.memset(p_raw_planes[:].rearrange("p g n -> p (g n)").bitcast(I32), 0)
+        nc.vector.memset(b_rows[0:127, :], 0.0)
+        nc.vector.memset(ones[:], 1.0)
         nc.vector.memset(c_planes[:].bitcast(I32), 0)
 
-        def load_x(i, g):
+        def load_x(i, passes):
             nc.sync.dma_start(
-                out=x_raw[i][g][:], in_=x_bytes[i].rearrange("(g p t) d -> g p t d", p=P, t=T)[g]
+                out=x_raw[i][:, passes].rearrange("p g t d -> p g (t d)"),
+                in_=x_bytes[i].rearrange("(g p t) d -> p g (t d)", p=P, t=T)[:, passes],
             )
 
-        def load_q(h, c):
+        def load_q(h, planes):
             nc.sync.dma_start(
-                out=q_raw[:, c, cols(h, 4), :],
-                in_=q[c].rearrange("(p j) m -> p j m", j=ROW_TILES)[:, cols(h, 4), :],
+                out=q_raw[:, planes, cols(h, 4), :].rearrange("p c j m -> p c (j m)"),
+                in_=q.rearrange("c (p h j) m -> h p c (j m)", h=2, j=4)[h][:, planes],
+            )
+
+        def load_p_planes(quad):
+            nc.sync.dma_start(
+                out=p_raw_planes[32 * quad : 32 * quad + 4, :, :].bitcast(I32),
+                in_=p_scales[:, cols(quad, 4), :].rearrange("g r n -> r g n").bitcast(I32),
+            )
+
+        def load_c_planes(quad):
+            nc.sync.dma_start(
+                out=c_planes[32 * quad : 32 * quad + 4, :].bitcast(I32),
+                in_=c_scales[0, cols(quad, 4), :].bitcast(I32),
             )
 
         nc.sync.dma_start(out=right[127:128, :], in_=om.rearrange("(o m) -> o m", o=1))
         nc.sync.dma_start(out=left[63:64, :], in_=nu.rearrange("(o n) -> o n", o=1))
-        nc.sync.dma_start(out=left[31:32, :], in_=b.rearrange("(o n) -> o n", o=1))
         nc.sync.dma_start(
             out=xs_rows[0:128:32, 0:16].rearrange("a (n j) -> a n j", j=BLOCKS),
             in_=x_scale.rearrange("i (g a) j -> a (i g) j", a=4),
         )
         nc.scalar.activation(out=warm_out[:], in_=warm_in[:], func=ACT.Abs_reciprocal_sqrt)
-        load_x(0, 0)
-        load_x(0, 1)
+        load_x(0, slice(0, 1))
+        load_x(0, slice(1, 2))
+        nc.sync.dma_start(out=b_rows[127:128, :], in_=b.rearrange("(o n) -> o n", o=1))
         nc.sync.dma_start(out=p_raw[:].bitcast(I32), in_=p_words.rearrange("g p n -> p g n").bitcast(I32))
-        load_q(0, 0)
-        load_q(0, 1)
+        load_q(0, slice(0, 1))
+        load_q(0, slice(1, 2))
         for quad in range(4):
-            nc.sync.dma_start(
-                out=p_raw_planes[32 * quad : 32 * quad + 4, :, :].bitcast(I32),
-                in_=p_scales[:, cols(quad, 4), :].rearrange("g r n -> r g n").bitcast(I32),
-            )
-        load_q(1, 0)
-        load_q(1, 1)
+            load_p_planes(quad)
+        load_q(1, slice(0, 1))
+        load_q(1, slice(1, 2))
         nc.sync.dma_start(out=c_codes[:].bitcast(I32), in_=c_words[0].bitcast(I32))
         for quad in range(4):
-            nc.sync.dma_start(
-                out=c_planes[32 * quad : 32 * quad + 4, :].bitcast(I32),
-                in_=c_scales[0, cols(quad, 4), :].bitcast(I32),
-            )
-        load_x(1, 0)
-        load_x(1, 1)
+            load_c_planes(quad)
+        load_x(1, slice(0, 2))
         make_identity(nc, identity[:])
 
         def difference(tm, n):
@@ -170,15 +189,11 @@ def tile_cauchytransferfunctionfilter_d2p_kernel(
         def spread_b(n):
             b_ps = bank(n, "b_ps")
             for t in range(T):
-                nc.tensor.matmul(b_ps[:, t : t + 1], lhsT=left[:, t::T], rhs=first_rows[:], start=True, stop=True)
+                nc.tensor.matmul(b_ps[:, t : t + 1], lhsT=b_rows[:, t::T], rhs=ones[:], start=True, stop=True)
             return b_ps
 
         def square(tm):
-            nc.scalar.activation(
-                out=squares[:, :, cols(tm)],
-                in_=difference_bank[tm][:].rearrange("p (t m) -> p t m", t=T),
-                func=ACT.Square,
-            )
+            nc.scalar.activation(out=squares[:, :, cols(tm)], in_=slices(difference_bank[tm][:]), func=ACT.Square)
 
         def inverse_root(half):
             ms = cols(half, 2 * P)
@@ -186,7 +201,11 @@ def tile_cauchytransferfunctionfilter_d2p_kernel(
                 out=roots[:, :, ms], in_=squares[:, :, ms], func=ACT.Abs_reciprocal_sqrt, bias=0.25
             )
 
-        def weight(half):
+        def inverse(half):
+            ms = cols(half, 2 * P)
+            nc.scalar.activation(out=inverses[:, :, ms], in_=roots[:, :, ms], func=ACT.Square)
+
+        def weight_from_roots(half):
             ms = cols(half, 2 * P)
             for t in range(T):
                 nc.vector.scalar_tensor_tensor(
@@ -198,45 +217,48 @@ def tile_cauchytransferfunctionfilter_d2p_kernel(
                     op1=MULT,
                 )
 
+        def weight_from_inverses(half):
+            ms = cols(half, 2 * P)
+            for t in range(T):
+                nc.vector.tensor_scalar(
+                    out=w[:, t, ms], in0=inverses[:, t, ms], scalar1=b_col[:, t : t + 1], scalar2=None, op0=MULT
+                )
+
         def g_imaginary(tm):
             nc.vector.tensor_tensor(
                 out=runs_of_words(g_bf[1][:, cols(tm), :]),
-                in0=by_runs(difference_bank[tm][:]),
-                in1=w[:, :, cols(tm)].rearrange("p t (g i) -> p g t i", i=RUN),
+                in0=by_runs(slices(difference_bank[tm][:])),
+                in1=by_runs(w[:, :, cols(tm)]),
                 op=MULT,
             )
 
-        def g_real(half, engine=None):
+        def g_real_scalar(half):
             ms = cols(half, 2 * P)
-            if engine:
-                engine.tensor_scalar(
-                    out=g_bf[0][:, ms, :],
-                    in0=w[:, :, ms].rearrange("p t m -> p m t"),
-                    scalar1=0.5,
-                    scalar2=0.0,
-                    op0=MULT,
-                    op1=ADD,
-                )
-            else:
-                nc.scalar.activation(
-                    out=runs_of_words(g_bf[0][:, ms, :]),
-                    in_=w[:, :, ms].rearrange("p t (g i) -> p g t i", i=RUN),
-                    func=ACT.Copy,
-                    scale=0.5,
-                )
-
-        def g_quantize(c):
-            nc.vector.quantize_mx(
-                out=g_codes[c][:].bitcast(E4M3), scales=g_scales[c][:], in_=g_bf[c][:].rearrange("p m t -> p (m t)")
+            nc.scalar.activation(
+                out=runs_of_words(g_bf[0][:, ms, :]), in_=by_runs(w[:, :, ms]), func=ACT.Copy, scale=0.5
             )
 
-        def transfer(blk, c):
-            k_ps = transfer_bank[blk, c] = passing_bank("transfer%d%d" % (blk, c))
+        def g_real_gpsimd(half):
+            ms = cols(half, 2 * P)
+            nc.gpsimd.tensor_scalar(
+                out=g_bf[0][:, ms, :],
+                in0=w[:, :, ms].rearrange("p t m -> p m t"),
+                scalar1=0.5,
+                scalar2=0.0,
+                op0=MULT,
+                op1=ADD,
+            )
+
+        def g_quantize(c):
+            quantize(g_codes[c][:], g_planes[c][:], g_bf[c][:].rearrange("p m t -> p (m t)"))
+
+        def transfer(blk, c, n):
+            k_ps = transfer_bank[blk, c] = bank(n, "transfer%d%d" % (blk, c))
             for t in range(T):
                 nc.tensor.matmul_mx(
                     out=k_ps[:, cols(t)],
                     lhsT=g_codes[c][:, cols(t)].bitcast(E4M3),
-                    lhsT_scale=g_scales[c][:, cols(t)],
+                    lhsT_scale=g_planes[c][:, cols(t)],
                     rhs=c_codes[:, cols(blk, 2 * P)].bitcast(E2M1),
                     rhs_scale=c_planes[:, cols(blk)],
                     start=True,
@@ -246,16 +268,16 @@ def tile_cauchytransferfunctionfilter_d2p_kernel(
         def keep_transfer(blk, c):
             nc.scalar.copy(out=transfer_kept[:, blk, c], in_=by_words(transfer_bank[blk, c][:]))
 
-        def permute_p_codes():
-            nc.vector.tensor_copy(
-                out=p_codes[:].bitcast(U16).rearrange("p g (t r i) -> p g r t i", t=T, i=LINE),
-                in_=p_raw[:].bitcast(U16).rearrange("p g (r i t) -> p g r t i", t=T, i=LINE),
+        def permute_p_codes(g, copy=nc.scalar.copy):
+            copy(
+                out=p_codes[:, g].bitcast(U16).rearrange("p (t r i) -> p r t i", t=T, i=LINE),
+                in_=p_raw[:, g].bitcast(U16).rearrange("p (r i t) -> p r t i", t=T, i=LINE),
             )
 
-        def permute_p_planes():
+        def permute_p_planes(g):
             nc.vector.tensor_copy(
-                out=p_planes[:].rearrange("p g (t n) -> p g t n", t=T),
-                in_=p_raw_planes[:].rearrange("p g (n t) -> p g t n", t=T),
+                out=p_planes[:, g].rearrange("p (t n) -> p t n", t=T),
+                in_=p_raw_planes[:, g].rearrange("p (n t) -> p t n", t=T),
             )
 
         def scales_to_columns():
@@ -267,73 +289,82 @@ def tile_cauchytransferfunctionfilter_d2p_kernel(
         def scales_to_rows():
             nc.vector.transpose(out=x_s[:], in_=xs_spread[:])
 
-        def x_widen(i, g):
-            nc.scalar.copy(
-                out=x_wide[g][:].rearrange("p t d -> p (t d)"),
-                in_=x_raw[i][g][:].rearrange("p t d -> p (t d)").bitcast(FP8),
-            )
-
-        def scale_block(i, g, blk, words, engine):
+        def x_scale_of(i, g, blk):
             column = BLOCKS * (2 * i + g) + blk
-            scale = x_s[:, column : column + 1]
-            values = (x_raw[i][g][:].bitcast(FP8) if engine == "vector" else x_wide[g][:])[:, :, cols(blk)]
-            runs = values.rearrange("p t (g i) -> p g t i", i=RUN)
-            if engine == "scalar":
-                nc.scalar.activation(out=runs_of_words(words), in_=runs, func=ACT.Copy, scale=scale)
-            elif engine == "vector":
-                nc.vector.tensor_scalar(out=runs_of_words(words), in0=runs, scalar1=scale, scalar2=None, op0=MULT)
-            else:
-                nc.gpsimd.tensor_scalar(
-                    out=words, in0=values.rearrange("p t d -> p d t"), scalar1=scale, scalar2=0.0, op0=MULT, op1=ADD
-                )
+            return x_s[:, column : column + 1]
 
-        def x_scale(i, g, blk, engine="vector"):
-            scale_block(i, g, blk, x_bf[i, blk // 2][:, g, cols(blk % 2), :], engine)
-
-        def x_quantize(i, h):
-            nc.vector.quantize_mx(
-                out=x_codes[i][h][:].rearrange("p g d -> p (g d)").bitcast(E4M3),
-                scales=x_planes[i][h][:].rearrange("p g d -> p (g d)"),
-                in_=x_bf[i, h][:].rearrange("p g d t -> p (g d t)"),
+        def x_scale_block(i, g, blk):
+            nc.vector.tensor_scalar(
+                out=runs_of_words(x_bf[i, g, blk]),
+                in0=by_runs(x_raw[i][:, g].bitcast(FP8)[:, :, cols(blk)]),
+                scalar1=x_scale_of(i, g, blk),
+                scalar2=None,
+                op0=MULT,
             )
 
-        def taken_over(name, shape):
-            return keep.tile(shape, BF16, name=name, tag="q_bf0", align_bytes=64)
-
-        def x_last_scale(g, blk, engine):
-            name = "x_last%d%d" % (g, blk)
-            make = taken_over if engine == "gpsimd" else lambda name, shape: sb(name, shape, BF16)
-            x_last[g, blk] = make(name, [P, P, T])
-            scale_block(1, g, blk, x_last[g, blk][:], engine)
-
-        def x_last_quantize(blk):
+        def x_on_vector(i, blk):
             for g in range(2):
-                nc.vector.quantize_mx(
-                    out=x_codes[1][1][:, g, cols(blk % 2)].bitcast(E4M3),
-                    scales=x_planes[1][1][:, g, cols(blk % 2)],
-                    in_=x_last[g, blk][:].rearrange("p d t -> p (d t)"),
-                )
+                x_scale_block(i, g, blk)
 
-        def analysis(i, blk):
-            u_ps = u_bank[i, blk] = bank(blk, "u%d%d" % (i, blk))
+        def x_widen(i, g, first, blocks=1):
+            wide = sb("x_wide%d%d%d" % (i, g, first), [P, T, blocks * P], BF16)
+            nc.scalar.copy(out=wide[:], in_=x_raw[i][:, g].bitcast(FP8)[:, :, P * first : P * (first + blocks)])
+            for n in range(blocks):
+                x_wide[i, g, first + n] = wide[:, :, cols(n)]
+
+        def x_scale_on_scalar(i, g, blk):
+            nc.scalar.activation(
+                out=runs_of_words(x_bf[i, g, blk]),
+                in_=by_runs(x_wide[i, g, blk]),
+                func=ACT.Copy,
+                scale=x_scale_of(i, g, blk),
+            )
+
+        def x_scale_on_gpsimd(i, g, blk, tag):
+            x_bf[i, g, blk] = sb("x_bf%d%d%d" % (i, g, blk), [P, P, T], BF16, tag=tag)[:]
+            nc.gpsimd.tensor_scalar(
+                out=x_bf[i, g, blk],
+                in0=x_wide[i, g, blk].rearrange("p t d -> p d t"),
+                scalar1=x_scale_of(i, g, blk),
+                scalar2=0.0,
+                op0=MULT,
+                op1=ADD,
+            )
+
+        def x_quantize(i, blk):
+            if (i, blk) in x_both:
+                quantize(
+                    x_codes[i, blk][:].rearrange("p g d -> p (g d)"),
+                    x_planes[i, blk][:].rearrange("p g d -> p (g d)"),
+                    x_both[i, blk][:].rearrange("p g d t -> p (g d t)"),
+                )
+            else:
+                for g in range(2):
+                    quantize(x_codes[i, blk][:, g], x_planes[i, blk][:, g], x_bf[i, g, blk].rearrange("p d t -> p (d t)"))
+
+        def analysis(i, blk, n):
+            u_ps = u_bank[i, blk] = bank(n, "u%d%d" % (i, blk))
             for t in range(T):
                 for g in range(2):
                     nc.tensor.matmul_mx(
                         out=u_ps[:, cols(t)],
                         lhsT=p_codes[:, g, cols(t, 2 * P)].bitcast(E2M1),
                         lhsT_scale=p_planes[:, g, cols(t)],
-                        rhs=x_codes[i][blk // 2][:, g, cols(blk % 2)].bitcast(E4M3),
-                        rhs_scale=x_planes[i][blk // 2][:, g, cols(blk % 2)],
+                        rhs=x_codes[i, blk][:, g].bitcast(E4M3),
+                        rhs_scale=x_planes[i, blk][:, g],
                         start=(g == 0),
                         stop=(g == 1),
                     )
 
+        def keep_u(i, blk):
+            u_kept[i, blk] = sb("u_kept%d%d" % (i, blk), [P, P, T], F32)
+            nc.scalar.copy(out=u_kept[i, blk][:], in_=by_words(u_bank[i, blk][:]))
+
         q_pairs = q_raw[:].rearrange("p c j m -> p (c j m)").bitcast(F32)
 
-        def q_turn(h, c, n):
+        def q_turn(h, c, banks):
             for pair in range(2):
-                name = "turned%d%d%d" % (h, c, pair)
-                turned = q_bank[h, c, pair] = bank(n + pair, name)
+                turned = q_bank[h, c, pair] = bank(banks[pair], "turned%d%d%d" % (h, c, pair))
                 for s in range(2):
                     first = (ROW_TILES * c + 4 * h + 2 * pair + s) * (M // 2)
                     for u in range(2):
@@ -344,69 +375,68 @@ def tile_cauchytransferfunctionfilter_d2p_kernel(
         def q_copy(h, c, pairs=range(2), copy=nc.scalar.copy):
             for pair in pairs:
                 copy(
-                    out=q_bf[h][:, c, cols(pair, 2)]
+                    out=q_bf[h, c][:, cols(pair, 2)]
                     .rearrange("p s r e -> p (s r e)")
                     .bitcast(F32)
                     .rearrange("p (s r u) -> p s r u", s=2, u=2),
                     in_=q_bank[h, c, pair][:].rearrange("p (s u r) -> p s r u", s=2, u=2),
                 )
 
-        def q_quantize(h):
-            nc.vector.quantize_mx(
-                out=q_codes[h][:].rearrange("p c r -> p (c r)").bitcast(E4M3),
-                scales=q_planes[h][:].rearrange("p c r -> p (c r)"),
-                in_=q_bf[h][:].rearrange("p c s r e -> p (c s r e)"),
-            )
+        def q_quantize(h, c):
+            quantize(q_codes[h, c][:], q_planes[h, c][:], q_bf[h, c][:].rearrange("p s r e -> p (s r e)"))
 
-        def filter_part(z, blk, c):
-            i, first = PIECES[z][:2]
+        def filter_part(z, n, c):
+            i, blk = PIECES[z][0], PIECES[z][1] + n
             nc.vector.tensor_tensor(
-                out=f_bf[z][:, c, cols(blk - first), :],
-                in0=by_words(u_bank[i, blk][:]),
-                in1=transfer_kept[:, blk, c],
-                op=MULT,
+                out=f_bf[z, c][:, n], in0=by_words(u_bank[i, blk][:]), in1=transfer_kept[:, blk, c], op=MULT
             )
 
-        def filter_block(z, blk):
-            for c in range(2):
-                filter_part(z, blk, c)
+        def filter_gpsimd(z, n, c, tag):
+            i, blk = PIECES[z][0], PIECES[z][1] + n
+            f_apart[z, n, c] = sb("f_apart%d%d%d" % (z, n, c), [P, P, T], BF16, tag=tag)
+            nc.gpsimd.tensor_tensor(out=f_apart[z, n, c][:], in0=u_kept[i, blk][:], in1=transfer_kept[:, blk, c], op=MULT)
 
-        def f_quantize(z):
-            nc.vector.quantize_mx(
-                out=f_codes[z][:].rearrange("p c d -> p (c d)").bitcast(E4M3),
-                scales=f_planes[z][:].rearrange("p c d -> p (c d)"),
-                in_=f_bf[z][:].rearrange("p c d t -> p (c d t)"),
-            )
+        def f_quantize(z, c, n=None):
+            ns = slice(0, PIECES[z][2]) if n is None else slice(n, n + 1)
+            ds = slice(P * ns.start, P * ns.stop)
+            values = f_apart[z, n, c][:] if (z, n, c) in f_apart else f_bf[z, c][:, ns].rearrange("p n d t -> p (n d) t")
+            quantize(f_codes[z][:, c, ds], f_planes[z][:, c, ds], values.rearrange("p d t -> p (d t)"))
 
-        def f_quantize_part(z, c):
-            nc.vector.quantize_mx(
-                out=f_codes[z][:, c, :].bitcast(E4M3),
-                scales=f_planes[z][:, c, :],
-                in_=f_bf[z][:, c].rearrange("p d t -> p (d t)"),
-            )
-
-        def synthesis(z, j0, tiles, held=None):
+        def synthesis(z, j0, n):
             width = P * PIECES[z][2]
-            name = "o%d%d" % (z, j0)
-            o_ps = out_bank[z, j0] = passing_bank(name) if held is None else bank(held, name)
-            for s in range(tiles):
+            o_ps = out_bank[z, j0] = bank(n, "o%d%d" % (z, j0))
+            for s in range(512 // width):
                 j = j0 + s
                 for c in range(2):
                     nc.tensor.matmul_mx(
                         out=o_ps[:, cols(s, width)],
-                        lhsT=q_codes[j // 4][:, c, cols(j % 4)].bitcast(E4M3),
-                        lhsT_scale=q_planes[j // 4][:, c, cols(j % 4)],
+                        lhsT=q_codes[j // 4, c][:, cols(j % 4)].bitcast(E4M3),
+                        lhsT_scale=q_planes[j // 4, c][:, cols(j % 4)],
                         rhs=f_codes[z][:, c, :].bitcast(E4M3),
                         rhs_scale=f_planes[z][:, c, :],
                         start=(c == 0),
                         stop=(c == 1),
                     )
 
-        def copy_out(z, j0, tiles, copy):
+        def synthesis_part(z, j0, c, n=None):
+            if n is not None:
+                out_bank[z, j0] = bank(n, "o%d%d" % (z, j0))
+            for s in range(2):
+                j = j0 + s
+                nc.tensor.matmul_mx(
+                    out=out_bank[z, j0][:, cols(s, 2 * P)],
+                    lhsT=q_codes[j // 4, c][:, cols(j % 4)].bitcast(E4M3),
+                    lhsT_scale=q_planes[j // 4, c][:, cols(j % 4)],
+                    rhs=f_codes[z][:, c, :].bitcast(E4M3),
+                    rhs_scale=f_planes[z][:, c, :],
+                    start=(n is not None and s == 0),
+                    stop=(n is None and s == 1),
+                )
+
+        def copy_out(z, j0, copy=nc.scalar.copy):
             width = P * PIECES[z][2]
             copy(
-                out=o_sb[z][:, j0 : j0 + tiles, :],
-                in_=out_bank[z, j0][:, 0 : tiles * width].rearrange("p (j d) -> p j d", d=width),
+                out=o_sb[z][:, j0 : j0 + 512 // width, :], in_=out_bank[z, j0][:].rearrange("p (j d) -> p j d", d=width)
             )
 
         def store(z, j0, tiles):
@@ -417,120 +447,137 @@ def tile_cauchytransferfunctionfilter_d2p_kernel(
                 in_=o_sb[z][:, rows, :],
             )
 
-        def output(z, j0, tiles, held=None, copy=nc.scalar.copy):
-            synthesis(z, j0, tiles, held)
-            copy_out(z, j0, tiles, copy)
-            store(z, j0, tiles)
+        def output(z, j0, copy=nc.scalar.copy):
+            copy_out(z, j0, copy)
+            store(z, j0, 512 // (P * PIECES[z][2]))
 
-        def output_half(z, h):
-            for j0 in (4 * h, 4 * h + 2):
-                synthesis(z, j0, 2)
-                copy_out(z, j0, 2, nc.scalar.copy)
-            store(z, 4 * h, 4)
-
-        def transfer_kept_for(blk):
-            for c in range(2):
-                transfer(blk, c)
-                keep_transfer(blk, c)
-
-        def f_quantize_parts(z):
-            for c in range(2):
-                f_quantize_part(z, c)
-
-        for tm, n in enumerate((4, 5, 6, 7)):
-            difference(tm, n)
+        for tm in range(T):
+            difference(tm, 4 + tm)
         b_ps = spread_b(0)
+        scales_to_columns()
+        scales_repeat()
+        scales_to_rows()
         for tm in range(T):
             square(tm)
         inverse_root(0)
         inverse_root(1)
-
-        scales_to_columns()
-        scales_repeat()
-        scales_to_rows()
         for blk in range(BLOCKS):
-            x_scale(0, 0, blk)
-        permute_p_codes()
+            x_scale_block(0, 0, blk)
         nc.vector.tensor_copy(out=b_col[:], in_=b_ps[:, 0:T])
         for blk in range(BLOCKS):
-            x_scale(0, 1, blk)
+            x_scale_block(0, 1, blk)
         x_quantize(0, 0)
-        permute_p_planes()
-        weight(0)
-        weight(1)
-        q_turn(0, 0, 0)
-        q_turn(0, 1, 2)
-        q_turn(1, 0, 4)
-        q_copy(0, 0)
-        q_copy(0, 1)
-        for tm in range(T):
-            difference(tm, tm)
-        q_turn(1, 1, 6)
-        g_real(0)
-        g_real(1, nc.gpsimd)
-        q_copy(1, 0)
-        x_widen(1, 0)
-        q_copy(1, 1, [1])
+        x_quantize(0, 1)
+        weight_from_roots(0)
+        permute_p_planes(0)
+        permute_p_planes(1)
+        weight_from_roots(1)
+        g_real_gpsimd(1)
         for tm in range(T):
             g_imaginary(tm)
-        q_copy(1, 1, [0], nc.vector.tensor_copy)
-        analysis(0, 0)
-        analysis(0, 1)
-        x_quantize(0, 1)
-        g_quantize(0)
+        q_turn(0, 0, (1, 2))
+        q_turn(0, 1, (3, 0))
+        q_copy(0, 0)
+        q_copy(0, 1)
+        permute_p_codes(0)
+        permute_p_codes(1)
+        g_real_scalar(0)
+        q_turn(1, 0, (1, 2))
+        q_turn(1, 1, (3, 0))
+        q_copy(1, 0)
+        q_copy(1, 1)
+        x_widen(1, 0, 0)
+        analysis(0, 0, 4)
+        analysis(0, 1, 5)
+        x_quantize(0, 2)
         g_quantize(1)
-        q_quantize(0)
-
-        x_bf[1, 0] = taken_over("x_bf10", [P, 2, 2 * P, T])
-        x_scale(1, 0, 0, "gpsimd")
-        x_widen(1, 1)
-        transfer_kept_for(0)
-        transfer_kept_for(1)
-        analysis(0, 2)
-        transfer(2, 0)
-        keep_transfer(2, 0)
-        x_scale(1, 1, 0, "scalar")
-        x_scale(1, 1, 1, "scalar")
-        transfer(2, 1)
+        g_quantize(0)
+        x_quantize(0, 3)
+        q_quantize(0, 0)
+        q_quantize(0, 1)
+        transfer(0, 1, 6)
+        transfer(1, 1, 7)
+        transfer(0, 0, 1)
+        transfer(1, 0, 2)
+        keep_transfer(0, 1)
+        keep_transfer(1, 1)
+        keep_transfer(0, 0)
+        keep_transfer(1, 0)
+        analysis(0, 2, 3)
+        transfer(2, 1, 6)
+        transfer(3, 1, 7)
+        analysis(0, 3, 0)
+        transfer(2, 0, 1)
+        transfer(3, 0, 2)
+        x_scale_on_gpsimd(1, 0, 0, "q_bf00")
+        for n, c in ((0, 1), (1, 1), (0, 0), (1, 0)):
+            filter_part(0, n, c)
         keep_transfer(2, 1)
-        analysis(0, 3)
-        transfer(3, 0)
-        transfer(3, 1)
-        filter_block(0, 0)
-        filter_block(0, 1)
-        f_quantize_parts(0)
-        x_scale(1, 0, 1)
-        q_quantize(1)
-        x_quantize(1, 0)
-        x_last_scale(1, 2, "gpsimd")
-        keep_transfer(3, 0)
-        output(0, 0, 2, held=0)
         keep_transfer(3, 1)
-        output(0, 2, 2, held=1)
-        x_last_scale(0, 2, "scalar")
-        output(0, 4, 2)
-        output(0, 6, 2)
-        x_last_scale(0, 3, "scalar")
-        x_last_scale(1, 3, "scalar")
-        analysis(1, 0)
-        analysis(1, 1)
-        filter_block(1, 2)
-        filter_block(1, 3)
-        f_quantize_parts(1)
-        x_last_quantize(2)
-        for j in range(0, 8, 2):
-            output(1, j, 2)
-        analysis(1, 2)
-        filter_block(2, 0)
-        filter_part(2, 1, 0)
-        x_last_quantize(3)
-        analysis(1, 3)
+        keep_transfer(2, 0)
+        keep_transfer(3, 0)
+        x_widen(1, 1, 2, 2)
+        x_scale_block(1, 1, 0)
+        f_quantize(0, 1)
+        f_quantize(0, 0)
+        x_on_vector(1, 1)
+        x_quantize(1, 0)
+        q_quantize(1, 0)
+        x_quantize(1, 1)
+        q_quantize(1, 1)
+        synthesis(0, 0, 6)
+        synthesis(0, 2, 7)
+        analysis(1, 0, 4)
+        analysis(1, 1, 5)
+        synthesis(0, 4, 1)
+        synthesis(0, 6, 2)
+        x_scale_on_gpsimd(1, 1, 2, "x_both11")
+        for n, c in ((0, 1), (1, 1), (0, 0), (1, 0)):
+            filter_part(1, n, c)
+        output(0, 0)
+        output(0, 2)
+        x_widen(1, 0, 2, 2)
+        x_scale_on_scalar(1, 0, 2)
+        output(0, 4)
+        output(0, 6)
+        x_scale_on_scalar(1, 0, 3)
+        x_scale_on_scalar(1, 1, 3)
+        x_quantize(1, 2)
+        f_quantize(1, 1)
+        f_quantize(1, 0)
+        analysis(1, 2, 3)
+        for j, n in zip(range(0, 8, 2), (6, 7, 1, 2)):
+            synthesis(1, j, n)
+            output(1, j)
+        filter_part(2, 0, 1)
         filter_part(2, 1, 1)
-        f_quantize_parts(2)
-        filter_block(3, 2)
-        filter_block(3, 3)
-        f_quantize_parts(3)
-        for j in range(0, 8, 2):
-            output(2, j, 2)
-        for m in range(4):
-            output(3, 2 * m, 2, held=m, copy=nc.vector.tensor_copy if m % 2 == 0 else nc.scalar.copy)
+        x_quantize(1, 3)
+        analysis(1, 3, 0)
+        filter_part(2, 0, 0)
+        f_quantize(2, 1)
+        filter_part(2, 1, 0)
+        f_quantize(2, 0, 0)
+        f_quantize(2, 0, 1)
+        filter_part(3, 0, 0)
+        filter_part(3, 1, 0)
+        filter_part(3, 0, 1)
+        f_quantize(3, 0)
+        filter_part(3, 1, 1)
+        f_quantize(3, 1, 0)
+        f_quantize(3, 1, 1)
+        synthesis_part(2, 0, 1, 6)
+        synthesis_part(2, 0, 0)
+        output(2, 0)
+        for j, n in zip(range(2, 8, 2), (7, 1, 2)):
+            synthesis(2, j, n)
+            output(2, j)
+        synthesis_part(3, 0, 0, 4)
+        synthesis_part(3, 2, 0, 5)
+        synthesis_part(3, 0, 1)
+        synthesis_part(3, 2, 1)
+        synthesis(3, 4, 6)
+        synthesis(3, 6, 7)
+        for j in (0, 4):
+            copy_out(3, j, nc.vector.tensor_copy)
+            copy_out(3, j + 2)
+            store(3, j, 4)

@@ -121,17 +121,17 @@ def tile_cauchytransferfunctionfilter_d2p_kernel(
 
         difference_bank, transfer_bank, q_bank, u_bank, out_bank = {}, {}, {}, {}, {}
 
-        nc.vector.memset(xs_rows[:], 0.0)
-        nc.vector.memset(p_raw_planes[:].rearrange("p g n -> p (g n)").bitcast(I32), 0)
         warm_in = sb("warm_in", [P, 1], F32)
         warm_out = sb("warm_out", [P, 1], F32)
         nc.vector.memset(warm_in[:], 1.0)
+        nc.vector.memset(xs_rows[:], 0.0)
         nc.vector.memset(left[0:63, :], 0.0)
         nc.vector.memset(left[64:128, :].bitcast(U32), ONES)
         nc.vector.memset(right[0:64, :].bitcast(U32), MINUS_ONES)
         nc.vector.memset(right[64:127, :], 0.0)
         nc.vector.memset(b_rows[0:127, :], 0.0)
         nc.vector.memset(ones[:], 1.0)
+        nc.vector.memset(p_raw_planes[:].rearrange("p g n -> p (g n)").bitcast(I32), 0)
         nc.vector.memset(c_planes[:].bitcast(I32), 0)
 
         def load_x(i, passes):
@@ -169,16 +169,16 @@ def tile_cauchytransferfunctionfilter_d2p_kernel(
         load_x(0, slice(1, 2))
         nc.sync.dma_start(out=b_rows[127:128, :], in_=b.rearrange("(o n) -> o n", o=1))
         nc.sync.dma_start(out=p_raw[:].bitcast(I32), in_=p_words.rearrange("g p n -> p g n").bitcast(I32))
-        load_q(0, slice(0, 1))
-        load_q(0, slice(1, 2))
         for quad in range(4):
             load_p_planes(quad)
+        load_q(0, slice(0, 1))
+        load_q(0, slice(1, 2))
         load_q(1, slice(0, 1))
-        load_q(1, slice(1, 2))
         nc.sync.dma_start(out=c_codes[:].bitcast(I32), in_=c_words[0].bitcast(I32))
         for quad in range(4):
             load_c_planes(quad)
         load_x(1, slice(0, 2))
+        load_q(1, slice(1, 2))
         make_identity(nc, identity[:])
 
         def difference(tm, n):
@@ -468,44 +468,46 @@ def tile_cauchytransferfunctionfilter_d2p_kernel(
             x_scale_block(0, 1, blk)
         x_quantize(0, 0)
         x_quantize(0, 1)
-        weight_from_roots(0)
         permute_p_planes(0)
         permute_p_planes(1)
+        weight_from_roots(0)
         weight_from_roots(1)
         g_real_gpsimd(1)
+        x_quantize(0, 2)
         for tm in range(T):
             g_imaginary(tm)
+        permute_p_codes(0)
+        permute_p_codes(1)
         q_turn(0, 0, (1, 2))
         q_turn(0, 1, (3, 0))
         q_copy(0, 0)
-        q_copy(0, 1)
-        permute_p_codes(0)
-        permute_p_codes(1)
         g_real_scalar(0)
+        q_copy(0, 1)
         q_turn(1, 0, (1, 2))
-        q_turn(1, 1, (3, 0))
-        q_copy(1, 0)
-        q_copy(1, 1)
-        x_widen(1, 0, 0)
         analysis(0, 0, 4)
         analysis(0, 1, 5)
-        x_quantize(0, 2)
+        q_copy(1, 0)
+        x_widen(1, 0, 0)
+        x_widen(1, 1, 2, 2)
+        x_widen(1, 0, 2, 2)
+        x_quantize(0, 3)
         g_quantize(1)
         g_quantize(0)
-        x_quantize(0, 3)
         q_quantize(0, 0)
         q_quantize(0, 1)
         transfer(0, 1, 6)
         transfer(1, 1, 7)
-        transfer(0, 0, 1)
-        transfer(1, 0, 2)
+        transfer(0, 0, 3)
+        transfer(1, 0, 0)
+        q_turn(1, 1, (1, 2))
         keep_transfer(0, 1)
         keep_transfer(1, 1)
         keep_transfer(0, 0)
         keep_transfer(1, 0)
-        analysis(0, 2, 3)
+        q_copy(1, 1)
         transfer(2, 1, 6)
         transfer(3, 1, 7)
+        analysis(0, 2, 3)
         analysis(0, 3, 0)
         transfer(2, 0, 1)
         transfer(3, 0, 2)
@@ -516,7 +518,6 @@ def tile_cauchytransferfunctionfilter_d2p_kernel(
         keep_transfer(3, 1)
         keep_transfer(2, 0)
         keep_transfer(3, 0)
-        x_widen(1, 1, 2, 2)
         x_scale_block(1, 1, 0)
         f_quantize(0, 1)
         f_quantize(0, 0)
@@ -536,7 +537,6 @@ def tile_cauchytransferfunctionfilter_d2p_kernel(
             filter_part(1, n, c)
         output(0, 0)
         output(0, 2)
-        x_widen(1, 0, 2, 2)
         x_scale_on_scalar(1, 0, 2)
         output(0, 4)
         output(0, 6)

@@ -30,7 +30,7 @@ FLOPS = 2 * (2 * M * N * D + B * M * S * D + 2 * B * S * M * D)
 
 
 PIECES = ((0, 0, 2), (0, 2, 2), (1, 0, 2), (1, 2, 2))
-ON_GPSIMD = ((1, 0, 0), (1, 1, 2))
+ON_GPSIMD = ((1, 1, 0), (1, 1, 2))
 APART = tuple((i, g, blk) for i, h, blk in ON_GPSIMD for g in range(2))
 
 
@@ -487,9 +487,7 @@ def tile_cauchytransferfunctionfilter_d2p_kernel(
         analysis(0, 0, 4)
         analysis(0, 1, 5)
         q_copy(1, 0)
-        x_widen(1, 0, 0)
-        x_widen(1, 1, 2, 2)
-        x_widen(1, 0, 2, 2)
+        x_widen(1, 1, 0, 4)
         x_quantize(0, 3)
         g_quantize(1)
         g_quantize(0)
@@ -505,23 +503,25 @@ def tile_cauchytransferfunctionfilter_d2p_kernel(
         keep_transfer(0, 0)
         keep_transfer(1, 0)
         q_copy(1, 1)
+        x_scale_on_scalar(1, 1, 1)
         transfer(2, 1, 6)
         transfer(3, 1, 7)
         analysis(0, 2, 3)
         analysis(0, 3, 0)
         transfer(2, 0, 1)
         transfer(3, 0, 2)
-        x_scale_on_gpsimd(1, 0, 0, "q_bf00")
+        x_scale_on_gpsimd(1, 1, 0, "q_bf00")
         for n, c in ((0, 1), (1, 1), (0, 0), (1, 0)):
             filter_part(0, n, c)
         keep_transfer(2, 1)
         keep_transfer(3, 1)
         keep_transfer(2, 0)
         keep_transfer(3, 0)
-        x_scale_block(1, 1, 0)
+        x_scale_block(1, 0, 0)
         f_quantize(0, 1)
         f_quantize(0, 0)
-        x_on_vector(1, 1)
+        x_scale_block(1, 0, 1)
+        x_scale_block(1, 0, 2)
         x_quantize(1, 0)
         q_quantize(1, 0)
         x_quantize(1, 1)
@@ -537,7 +537,7 @@ def tile_cauchytransferfunctionfilter_d2p_kernel(
             filter_part(1, n, c)
         output(0, 0)
         output(0, 2)
-        x_scale_on_scalar(1, 0, 2)
+        x_widen(1, 0, 3)
         output(0, 4)
         output(0, 6)
         x_scale_on_scalar(1, 0, 3)

@@ -30,7 +30,7 @@ FLOPS = 2 * (2 * M * N * D + B * M * S * D + 2 * B * S * M * D)
 
 
 PIECES = ((0, 0, 2), (0, 2, 2), (1, 0, 2), (1, 2, 2))
-ON_GPSIMD = ((1, 1, 0), (1, 1, 2))
+ON_GPSIMD = ((1, 1, 0), (1, 1, 1), (1, 1, 2), (1, 1, 3))
 APART = tuple((i, g, blk) for i, h, blk in ON_GPSIMD for g in range(2))
 
 
@@ -124,7 +124,7 @@ def tile_cauchytransferfunctionfilter_d2p_kernel(
         warm_in = sb("warm_in", [P, 1], F32)
         warm_out = sb("warm_out", [P, 1], F32)
         nc.vector.memset(warm_in[:], 1.0)
-        nc.vector.memset(xs_rows[:], 0.0)
+        nc.gpsimd.memset(xs_rows[:], 0.0)
         nc.vector.memset(left[0:63, :], 0.0)
         nc.vector.memset(left[64:128, :].bitcast(U32), ONES)
         nc.vector.memset(right[0:64, :].bitcast(U32), MINUS_ONES)
@@ -274,10 +274,10 @@ def tile_cauchytransferfunctionfilter_d2p_kernel(
                 in_=p_raw[:, g].bitcast(U16).rearrange("p (r i t) -> p r t i", t=T, i=LINE),
             )
 
-        def permute_p_planes(g):
+        def permute_p_planes():
             nc.vector.tensor_copy(
-                out=p_planes[:, g].rearrange("p (t n) -> p t n", t=T),
-                in_=p_raw_planes[:, g].rearrange("p (n t) -> p t n", t=T),
+                out=p_planes[:].rearrange("p g (t n) -> p g t n", t=T),
+                in_=p_raw_planes[:].rearrange("p g (n t) -> p g t n", t=T),
             )
 
         def scales_to_columns():
@@ -320,7 +320,7 @@ def tile_cauchytransferfunctionfilter_d2p_kernel(
                 scale=x_scale_of(i, g, blk),
             )
 
-        def x_scale_on_gpsimd(i, g, blk, tag):
+        def x_scale_on_gpsimd(i, g, blk, tag=None):
             x_bf[i, g, blk] = sb("x_bf%d%d%d" % (i, g, blk), [P, P, T], BF16, tag=tag)[:]
             nc.gpsimd.tensor_scalar(
                 out=x_bf[i, g, blk],
@@ -468,16 +468,17 @@ def tile_cauchytransferfunctionfilter_d2p_kernel(
             x_scale_block(0, 1, blk)
         x_quantize(0, 0)
         x_quantize(0, 1)
-        permute_p_planes(0)
-        permute_p_planes(1)
+        permute_p_planes()
         weight_from_roots(0)
-        weight_from_roots(1)
-        g_real_gpsimd(1)
+        permute_p_codes(0)
+        inverse(1)
+        permute_p_codes(1)
         x_quantize(0, 2)
+        weight_from_inverses(1)
+        g_real_gpsimd(1)
+        x_quantize(0, 3)
         for tm in range(T):
             g_imaginary(tm)
-        permute_p_codes(0)
-        permute_p_codes(1)
         q_turn(0, 0, (1, 2))
         q_turn(0, 1, (3, 0))
         q_copy(0, 0)
@@ -488,9 +489,10 @@ def tile_cauchytransferfunctionfilter_d2p_kernel(
         analysis(0, 1, 5)
         q_copy(1, 0)
         x_widen(1, 1, 0, 4)
-        x_quantize(0, 3)
+        x_scale_block(1, 0, 0)
         g_quantize(1)
         g_quantize(0)
+        x_scale_block(1, 0, 1)
         q_quantize(0, 0)
         q_quantize(0, 1)
         transfer(0, 1, 6)
@@ -503,7 +505,6 @@ def tile_cauchytransferfunctionfilter_d2p_kernel(
         keep_transfer(0, 0)
         keep_transfer(1, 0)
         q_copy(1, 1)
-        x_scale_on_scalar(1, 1, 1)
         transfer(2, 1, 6)
         transfer(3, 1, 7)
         analysis(0, 2, 3)
@@ -511,18 +512,16 @@ def tile_cauchytransferfunctionfilter_d2p_kernel(
         transfer(2, 0, 1)
         transfer(3, 0, 2)
         x_scale_on_gpsimd(1, 1, 0, "q_bf00")
+        x_scale_on_gpsimd(1, 1, 1)
         for n, c in ((0, 1), (1, 1), (0, 0), (1, 0)):
             filter_part(0, n, c)
         keep_transfer(2, 1)
         keep_transfer(3, 1)
         keep_transfer(2, 0)
         keep_transfer(3, 0)
-        x_scale_block(1, 0, 0)
+        x_quantize(1, 0)
         f_quantize(0, 1)
         f_quantize(0, 0)
-        x_scale_block(1, 0, 1)
-        x_scale_block(1, 0, 2)
-        x_quantize(1, 0)
         q_quantize(1, 0)
         x_quantize(1, 1)
         q_quantize(1, 1)
@@ -532,16 +531,17 @@ def tile_cauchytransferfunctionfilter_d2p_kernel(
         analysis(1, 1, 5)
         synthesis(0, 4, 1)
         synthesis(0, 6, 2)
-        x_scale_on_gpsimd(1, 1, 2, "x_both11")
+        x_scale_on_gpsimd(1, 1, 2, "x_bf101")
+        x_scale_on_gpsimd(1, 1, 3)
         for n, c in ((0, 1), (1, 1), (0, 0), (1, 0)):
             filter_part(1, n, c)
+        x_widen(1, 0, 2, 2)
         output(0, 0)
+        x_scale_on_scalar(1, 0, 2)
         output(0, 2)
-        x_widen(1, 0, 3)
         output(0, 4)
         output(0, 6)
         x_scale_on_scalar(1, 0, 3)
-        x_scale_on_scalar(1, 1, 3)
         x_quantize(1, 2)
         f_quantize(1, 1)
         f_quantize(1, 0)

@@ -468,11 +468,11 @@ def tile_cauchytransferfunctionfilter_d2p_kernel(
             x_scale_block(0, 1, blk)
         x_quantize(0, 0)
         x_quantize(0, 1)
+        permute_p_codes(0, nc.vector.tensor_copy)
+        permute_p_codes(1, nc.vector.tensor_copy)
         permute_p_planes()
         weight_from_roots(0)
-        permute_p_codes(0)
         inverse(1)
-        permute_p_codes(1)
         x_quantize(0, 2)
         weight_from_inverses(1)
         g_real_gpsimd(1)

@@ -113,7 +113,7 @@ def tile_cauchytransferfunctionfilter_d2p_kernel(
         q_codes = {hc: sb("q_codes%d%d" % hc, [P, 4 * P], U32) for hc in q_bf}
         q_planes = {hc: sb("q_planes%d%d" % hc, [P, 4 * P], U8) for hc in q_bf}
 
-        f_bf = {(z, c): sb("f_bf%d%d" % (z, c), [P, PIECES[z][2], P, T], BF16) for z in range(len(PIECES)) for c in range(2)}
+        f_bf = [sb("f_bf%d" % z, [P, 2, PIECES[z][2], P, T], BF16) for z in range(len(PIECES))]
         f_codes = [sb("f_codes%d" % z, [P, 2, P * PIECES[z][2]], U32) for z in range(len(PIECES))]
         f_planes = [sb("f_planes%d" % z, [P, 2, P * PIECES[z][2]], U8) for z in range(len(PIECES))]
         o_sb = [sb("o_sb%d" % z, [P, ROW_TILES, P * PIECES[z][2]], F32) for z in range(len(PIECES))]
@@ -205,8 +205,8 @@ def tile_cauchytransferfunctionfilter_d2p_kernel(
             ms = cols(half, 2 * P)
             nc.scalar.activation(out=inverses[:, :, ms], in_=roots[:, :, ms], func=ACT.Square)
 
-        def weight_from_roots(half):
-            ms = cols(half, 2 * P)
+        def weight_from_roots(half=None):
+            ms = slice(0, M) if half is None else cols(half, 2 * P)
             for t in range(T):
                 nc.vector.scalar_tensor_tensor(
                     out=w[:, t, ms],
@@ -388,7 +388,16 @@ def tile_cauchytransferfunctionfilter_d2p_kernel(
         def filter_part(z, n, c):
             i, blk = PIECES[z][0], PIECES[z][1] + n
             nc.vector.tensor_tensor(
-                out=f_bf[z, c][:, n], in0=by_words(u_bank[i, blk][:]), in1=transfer_kept[:, blk, c], op=MULT
+                out=f_bf[z][:, c, n], in0=by_words(u_bank[i, blk][:]), in1=transfer_kept[:, blk, c], op=MULT
+            )
+
+        def filter_both(z, n):
+            i, blk = PIECES[z][0], PIECES[z][1] + n
+            nc.vector.tensor_tensor(
+                out=f_bf[z][:, :, n],
+                in0=by_words(u_bank[i, blk][:]).unsqueeze(1).to_broadcast([P, 2, P, T]),
+                in1=transfer_kept[:, blk],
+                op=MULT,
             )
 
         def filter_gpsimd(z, n, c, tag):
@@ -399,7 +408,7 @@ def tile_cauchytransferfunctionfilter_d2p_kernel(
         def f_quantize(z, c, n=None):
             ns = slice(0, PIECES[z][2]) if n is None else slice(n, n + 1)
             ds = slice(P * ns.start, P * ns.stop)
-            values = f_apart[z, n, c][:] if (z, n, c) in f_apart else f_bf[z, c][:, ns].rearrange("p n d t -> p (n d) t")
+            values = f_apart[z, n, c][:] if (z, n, c) in f_apart else f_bf[z][:, c, ns].rearrange("p n d t -> p (n d) t")
             quantize(f_codes[z][:, c, ds], f_planes[z][:, c, ds], values.rearrange("p d t -> p (d t)"))
 
         def synthesis(z, j0, n):
@@ -439,10 +448,10 @@ def tile_cauchytransferfunctionfilter_d2p_kernel(
                 out=o_sb[z][:, j0 : j0 + 512 // width, :], in_=out_bank[z, j0][:].rearrange("p (j d) -> p j d", d=width)
             )
 
-        def store(z, j0, tiles):
+        def store(z, j0, tiles, queue=nc.sync):
             i, first, blocks = PIECES[z]
             rows = slice(j0, j0 + tiles)
-            nc.sync.dma_start(
+            queue.dma_start(
                 out=out[i].rearrange("(p j) d -> p j d", j=ROW_TILES)[:, rows, P * first : P * (first + blocks)],
                 in_=o_sb[z][:, rows, :],
             )
@@ -496,28 +505,29 @@ def tile_cauchytransferfunctionfilter_d2p_kernel(
         q_quantize(0, 0)
         q_quantize(0, 1)
         transfer(0, 1, 6)
-        transfer(1, 1, 7)
-        transfer(0, 0, 3)
+        transfer(0, 0, 7)
+        transfer(1, 1, 3)
         transfer(1, 0, 0)
         q_turn(1, 1, (1, 2))
         keep_transfer(0, 1)
-        keep_transfer(1, 1)
         keep_transfer(0, 0)
+        keep_transfer(1, 1)
         keep_transfer(1, 0)
         q_copy(1, 1)
         transfer(2, 1, 6)
-        transfer(3, 1, 7)
+        transfer(2, 0, 7)
         analysis(0, 2, 3)
         analysis(0, 3, 0)
-        transfer(2, 0, 1)
+        transfer(3, 1, 1)
         transfer(3, 0, 2)
         x_scale_on_gpsimd(1, 1, 0, "q_bf00")
         x_scale_on_gpsimd(1, 1, 1)
-        for n, c in ((0, 1), (1, 1), (0, 0), (1, 0)):
-            filter_part(0, n, c)
+        filter_part(0, 0, 1)
+        filter_part(0, 0, 0)
+        filter_both(0, 1)
         keep_transfer(2, 1)
-        keep_transfer(3, 1)
         keep_transfer(2, 0)
+        keep_transfer(3, 1)
         keep_transfer(3, 0)
         x_quantize(1, 0)
         f_quantize(0, 1)
@@ -533,8 +543,8 @@ def tile_cauchytransferfunctionfilter_d2p_kernel(
         synthesis(0, 6, 2)
         x_scale_on_gpsimd(1, 1, 2, "x_bf101")
         x_scale_on_gpsimd(1, 1, 3)
-        for n, c in ((0, 1), (1, 1), (0, 0), (1, 0)):
-            filter_part(1, n, c)
+        filter_both(1, 0)
+        filter_both(1, 1)
         x_widen(1, 0, 2, 2)
         output(0, 0)
         x_scale_on_scalar(1, 0, 2)
@@ -549,11 +559,10 @@ def tile_cauchytransferfunctionfilter_d2p_kernel(
         for j, n in zip(range(0, 8, 2), (6, 7, 1, 2)):
             synthesis(1, j, n)
             output(1, j)
-        filter_part(2, 0, 1)
+        filter_both(2, 0)
         filter_part(2, 1, 1)
         x_quantize(1, 3)
         analysis(1, 3, 0)
-        filter_part(2, 0, 0)
         f_quantize(2, 1)
         filter_part(2, 1, 0)
         f_quantize(2, 0, 0)
@@ -577,7 +586,9 @@ def tile_cauchytransferfunctionfilter_d2p_kernel(
         synthesis_part(3, 2, 1)
         synthesis(3, 4, 6)
         synthesis(3, 6, 7)
-        for j in (0, 4):
-            copy_out(3, j, nc.vector.tensor_copy)
-            copy_out(3, j + 2)
-            store(3, j, 4)
+        output(3, 0, nc.vector.tensor_copy)
+        copy_out(3, 2)
+        store(3, 2, 2, nc.scalar)
+        output(3, 4, nc.vector.tensor_copy)
+        copy_out(3, 6)
+        store(3, 6, 2, nc.scalar)

@@ -124,7 +124,7 @@ def tile_cauchytransferfunctionfilter_d2p_kernel(
         warm_in = sb("warm_in", [P, 1], F32)
         warm_out = sb("warm_out", [P, 1], F32)
         nc.vector.memset(warm_in[:], 1.0)
-        nc.gpsimd.memset(xs_rows[:], 0.0)
+        nc.vector.memset(xs_rows[:], 0.0)
         nc.vector.memset(left[0:63, :], 0.0)
         nc.vector.memset(left[64:128, :].bitcast(U32), ONES)
         nc.vector.memset(right[0:64, :].bitcast(U32), MINUS_ONES)

from contextlib import ExitStack

import concourse.mybir as mybir
from concourse.masks import make_identity

F32 = mybir.dt.float32
BF16 = mybir.dt.bfloat16
U32 = mybir.dt.uint32
I32 = mybir.dt.int32
U16 = mybir.dt.uint16
U8 = mybir.dt.uint8
FP8 = mybir.dt.float8_e4m3fn
E4M3 = mybir.dt.float8_e4m3fn_x4
E2M1 = mybir.dt.float4_e2m1fn_x4
MULT = mybir.AluOpType.mult
ADD = mybir.AluOpType.add
ACT = mybir.ActivationFunctionType

B, S, D, M, N = 2, 1024, 512, 512, 512
P = 128
T = 4
RUN = 4
LINE = 8
BLOCKS = D // P
ROW_TILES = S // P
ONES = 0x3F803F80
MINUS_ONES = 0xBF80BF80

FLOPS = 2 * (2 * M * N * D + B * M * S * D + 2 * B * S * M * D)


PIECES = ((0, 0, 2), (0, 2, 2), (1, 0, 2), (1, 2, 2))
ON_GPSIMD = ((1, 1, 0), (1, 1, 1), (1, 1, 2), (1, 1, 3))
APART = tuple((i, g, blk) for i, h, blk in ON_GPSIMD for g in range(2))


def tile_cauchytransferfunctionfilter_d2p_kernel(
    tc, x_bytes, x_scale, p_words, p_scales, om, nu, b, c_words, c_scales, q, out
):
    nc = tc.nc
    with ExitStack() as ctx:
        keep = ctx.enter_context(tc.tile_pool(name="keep", bufs=1))
        psum = ctx.enter_context(tc.psum_pool(name="psum", bufs=1))
        ctx.enter_context(tc.manual_schedule())

        def bank(n, name):
            return psum.tile([P, 512], F32, tag="bank%d" % n, name=name)

        def sb(name, shape, dt, tag=None):
            return keep.tile(shape, dt, name=name, tag=tag or name, align_bytes=64)

        def cols(n, width=P):
            return slice(width * n, width * n + width)

        def by_runs(ap, run=RUN):
            return ap.rearrange("p t (g i) -> p g t i", i=run)

        def slices(ap):
            return ap.rearrange("p (t d) -> p t d", t=T)

        def by_words(ap):
            return ap.rearrange("p (t d) -> p d t", t=T)

        def runs_of_words(ap, run=RUN):
            return ap.rearrange("p (g i) t -> p g t i", i=run)

        def quantize(codes, planes, values):
            nc.vector.quantize_mx(out=codes.bitcast(E4M3), scales=planes, in_=values)

        left = sb("left", [P, N], BF16)
        right = sb("right", [P, M], BF16)
        b_rows = sb("b_rows", [P, N], BF16)
        ones = sb("ones", [P, 1], BF16)
        b_col = sb("b_col", [P, T], F32)
        squares = sb("squares", [P, T, M], F32)
        roots = sb("roots", [P, T, M], F32)
        inverses = sb("inverses", [P, T, M], F32)
        w = sb("w", [P, T, M], F32)
        g_bf = [sb("g_bf%d" % c, [P, M, T], BF16) for c in range(2)]
        g_codes = [sb("g_codes%d" % c, [P, M], U32) for c in range(2)]
        g_planes = [sb("g_planes%d" % c, [P, M], U8) for c in range(2)]

        c_codes = sb("c_codes", [P, 2 * D], U8)
        c_planes = sb("c_planes", [P, D], U8)
        transfer_kept = sb("transfer_kept", [P, BLOCKS, 2, P, T], F32)

        p_raw = sb("p_raw", [P, 2, 2 * M], U8)
        p_raw_planes = sb("p_raw_planes", [P, 2, M], U8)
        p_codes = sb("p_codes", [P, 2, 2 * M], U8)
        p_planes = sb("p_planes", [P, 2, M], U8)

        x_raw = [sb("x_raw%d" % i, [P, 2, T, D], U8) for i in range(B)]
        x_bf = {
            (i, g, blk): sb("x_bf%d%d%d" % (i, g, blk), [P, P, T], BF16)[:] for i, g, blk in APART if (i, g, blk) not in ON_GPSIMD
        }
        x_both = {}
        for i in range(B):
            for blk in range(BLOCKS):
                if (i, 0, blk) not in APART:
                    x_both[i, blk] = sb("x_both%d%d" % (i, blk), [P, 2, P, T], BF16)
                    for g in range(2):
                        x_bf[i, g, blk] = x_both[i, blk][:, g]
        x_codes = {(i, blk): sb("x_codes%d%d" % (i, blk), [P, 2, P], U32) for i in range(B) for blk in range(BLOCKS)}
        x_planes = {ib: sb("x_planes%d%d" % ib, [P, 2, P], U8) for ib in x_codes}
        xs_rows = sb("xs_rows", [P, 32], F32)
        xs_columns = sb("xs_columns", [P, 32], F32)
        xs_spread = sb("xs_spread", [P, 32], F32)
        x_s = sb("x_s", [P, 32], F32)

        identity = sb("identity", [P, P], F32)
        q_raw = sb("q_raw", [P, 2, ROW_TILES, M], BF16)
        q_bf = {(h, c): sb("q_bf%d%d" % (h, c), [P, 4, P, T], BF16) for h in range(2) for c in range(2)}
        q_codes = {hc: sb("q_codes%d%d" % hc, [P, 4 * P], U32) for hc in q_bf}
        q_planes = {hc: sb("q_planes%d%d" % hc, [P, 4 * P], U8) for hc in q_bf}

        f_bf = [sb("f_bf%d" % z, [P, 2, PIECES[z][2], P, T], BF16) for z in range(len(PIECES))]
        f_codes = [sb("f_codes%d" % z, [P, 2, P * PIECES[z][2]], U32) for z in range(len(PIECES))]
        f_planes = [sb("f_planes%d" % z, [P, 2, P * PIECES[z][2]], U8) for z in range(len(PIECES))]
        o_sb = [sb("o_sb%d" % z, [P, ROW_TILES, P * PIECES[z][2]], F32) for z in range(len(PIECES))]
        x_wide, u_kept, f_apart = {}, {}, {}

        difference_bank, transfer_bank, q_bank, u_bank, out_bank = {}, {}, {}, {}, {}

        warm_in = sb("warm_in", [P, 1], F32)
        warm_out = sb("warm_out", [P, 1], F32)
        nc.vector.memset(warm_in[:], 1.0)
        nc.vector.memset(xs_rows[:], 0.0)
        nc.vector.memset(left[0:63, :], 0.0)
        nc.vector.memset(left[64:128, :].bitcast(U32), ONES)
        nc.vector.memset(right[0:64, :].bitcast(U32), MINUS_ONES)
        nc.vector.memset(right[64:127, :], 0.0)
        nc.vector.memset(b_rows[0:127, :], 0.0)
        nc.vector.memset(ones[:], 1.0)
        nc.vector.memset(p_raw_planes[:].rearrange("p g n -> p (g n)").bitcast(I32), 0)
        nc.vector.memset(c_planes[:].bitcast(I32), 0)

        def load_x(i, passes):
            nc.sync.dma_start(
                out=x_raw[i][:, passes].rearrange("p g t d -> p g (t d)"),
                in_=x_bytes[i].rearrange("(g p t) d -> p g (t d)", p=P, t=T)[:, passes],
            )

        def load_q(h, planes):
            nc.sync.dma_start(
                out=q_raw[:, planes, cols(h, 4), :].rearrange("p c j m -> p c (j m)"),
                in_=q.rearrange("c (p h j) m -> h p c (j m)", h=2, j=4)[h][:, planes],
            )

        def load_p_planes(quad):
            nc.sync.dma_start(
                out=p_raw_planes[32 * quad : 32 * quad + 4, :, :].bitcast(I32),
                in_=p_scales[:, cols(quad, 4), :].rearrange("g r n -> r g n").bitcast(I32),
            )

        def load_c_planes(quad):
            nc.sync.dma_start(
                out=c_planes[32 * quad : 32 * quad + 4, :].bitcast(I32),
                in_=c_scales[0, cols(quad, 4), :].bitcast(I32),
            )

        nc.sync.dma_start(out=right[127:128, :], in_=om.rearrange("(o m) -> o m", o=1))
        nc.sync.dma_start(out=left[63:64, :], in_=nu.rearrange("(o n) -> o n", o=1))
        nc.sync.dma_start(
            out=xs_rows[0:128:32, 0:16].rearrange("a (n j) -> a n j", j=BLOCKS),
            in_=x_scale.rearrange("i (g a) j -> a (i g) j", a=4),
        )
        nc.scalar.activation(out=warm_out[:], in_=warm_in[:], func=ACT.Abs_reciprocal_sqrt)
        load_x(0, slice(0, 1))
        load_x(0, slice(1, 2))
        nc.sync.dma_start(out=b_rows[127:128, :], in_=b.rearrange("(o n) -> o n", o=1))
        nc.sync.dma_start(out=p_raw[:].bitcast(I32), in_=p_words.rearrange("g p n -> p g n").bitcast(I32))
        for quad in range(4):
            load_p_planes(quad)
        load_q(0, slice(0, 1))
        load_q(0, slice(1, 2))
        load_q(1, slice(0, 1))
        nc.sync.dma_start(out=c_codes[:].bitcast(I32), in_=c_words[0].bitcast(I32))
        for quad in range(4):
            load_c_planes(quad)
        load_x(1, slice(0, 2))
        load_q(1, slice(1, 2))
        make_identity(nc, identity[:])

        def difference(tm, n):
            d = difference_bank[tm] = bank(n, "difference%d%d" % (tm, n))
            for t in range(T):
                nc.tensor.matmul(d[:, cols(t)], lhsT=left[:, t::T], rhs=right[:, tm::T], start=True, stop=True)

        def spread_b(n):
            b_ps = bank(n, "b_ps")
            for t in range(T):
                nc.tensor.matmul(b_ps[:, t : t + 1], lhsT=b_rows[:, t::T], rhs=ones[:], start=True, stop=True)
            return b_ps

        def square(tm):
            nc.scalar.activation(out=squares[:, :, cols(tm)], in_=slices(difference_bank[tm][:]), func=ACT.Square)

        def inverse_root(half):
            ms = cols(half, 2 * P)
            nc.scalar.activation(
                out=roots[:, :, ms], in_=squares[:, :, ms], func=ACT.Abs_reciprocal_sqrt, bias=0.25
            )

        def inverse(half):
            ms = cols(half, 2 * P)
            nc.scalar.activation(out=inverses[:, :, ms], in_=roots[:, :, ms], func=ACT.Square)

        def weight_from_roots(half=None):
            ms = slice(0, M) if half is None else cols(half, 2 * P)
            for t in range(T):
                nc.vector.scalar_tensor_tensor(
                    out=w[:, t, ms],
                    in0=roots[:, t, ms],
                    scalar=b_col[:, t : t + 1],
                    in1=roots[:, t, ms],
                    op0=MULT,
                    op1=MULT,
                )

        def weight_from_inverses(half):
            ms = cols(half, 2 * P)
            for t in range(T):
                nc.vector.tensor_scalar(
                    out=w[:, t, ms], in0=inverses[:, t, ms], scalar1=b_col[:, t : t + 1], scalar2=None, op0=MULT
                )

        def g_imaginary(tm):
            nc.vector.tensor_tensor(
                out=runs_of_words(g_bf[1][:, cols(tm), :]),
                in0=by_runs(slices(difference_bank[tm][:])),
                in1=by_runs(w[:, :, cols(tm)]),
                op=MULT,
            )

        def g_real_scalar(half):
            ms = cols(half, 2 * P)
            nc.scalar.activation(
                out=runs_of_words(g_bf[0][:, ms, :]), in_=by_runs(w[:, :, ms]), func=ACT.Copy, scale=0.5
            )

        def g_real_gpsimd(half):
            ms = cols(half, 2 * P)
            nc.gpsimd.tensor_scalar(
                out=g_bf[0][:, ms, :],
                in0=w[:, :, ms].rearrange("p t m -> p m t"),
                scalar1=0.5,
                scalar2=0.0,
                op0=MULT,
                op1=ADD,
            )

        def g_quantize(c):
            quantize(g_codes[c][:], g_planes[c][:], g_bf[c][:].rearrange("p m t -> p (m t)"))

        def transfer(blk, c, n):
            k_ps = transfer_bank[blk, c] = bank(n, "transfer%d%d" % (blk, c))
            for t in range(T):
                nc.tensor.matmul_mx(
                    out=k_ps[:, cols(t)],
                    lhsT=g_codes[c][:, cols(t)].bitcast(E4M3),
                    lhsT_scale=g_planes[c][:, cols(t)],
                    rhs=c_codes[:, cols(blk, 2 * P)].bitcast(E2M1),
                    rhs_scale=c_planes[:, cols(blk)],
                    start=True,
                    stop=True,
                )

        def keep_transfer(blk, c):
            nc.scalar.copy(out=transfer_kept[:, blk, c], in_=by_words(transfer_bank[blk, c][:]))

        def permute_p_codes(g, copy=nc.scalar.copy):
            copy(
                out=p_codes[:, g].bitcast(U16).rearrange("p (t r i) -> p r t i", t=T, i=LINE),
                in_=p_raw[:, g].bitcast(U16).rearrange("p (r i t) -> p r t i", t=T, i=LINE),
            )

        def permute_p_planes():
            nc.vector.tensor_copy(
                out=p_planes[:].rearrange("p g (t n) -> p g t n", t=T),
                in_=p_raw_planes[:].rearrange("p g (n t) -> p g t n", t=T),
            )

        def scales_to_columns():
            nc.vector.transpose(out=xs_columns[:], in_=xs_rows[:])

        def scales_repeat():
            nc.vector.tensor_copy(out=xs_spread[:], in_=xs_columns[:, 0:1].to_broadcast([P, 32]))

        def scales_to_rows():
            nc.vector.transpose(out=x_s[:], in_=xs_spread[:])

        def x_scale_of(i, g, blk):
            column = BLOCKS * (2 * i + g) + blk
            return x_s[:, column : column + 1]

        def x_scale_block(i, g, blk):
            nc.vector.tensor_scalar(
                out=runs_of_words(x_bf[i, g, blk]),
                in0=by_runs(x_raw[i][:, g].bitcast(FP8)[:, :, cols(blk)]),
                scalar1=x_scale_of(i, g, blk),
                scalar2=None,
                op0=MULT,
            )

        def x_on_vector(i, blk):
            for g in range(2):
                x_scale_block(i, g, blk)

        def x_widen(i, g, first, blocks=1):
            wide = sb("x_wide%d%d%d" % (i, g, first), [P, T, blocks * P], BF16)
            nc.scalar.copy(out=wide[:], in_=x_raw[i][:, g].bitcast(FP8)[:, :, P * first : P * (first + blocks)])
            for n in range(blocks):
                x_wide[i, g, first + n] = wide[:, :, cols(n)]

        def x_scale_on_scalar(i, g, blk):
            nc.scalar.activation(
                out=runs_of_words(x_bf[i, g, blk]),
                in_=by_runs(x_wide[i, g, blk]),
                func=ACT.Copy,
                scale=x_scale_of(i, g, blk),
            )

        def x_scale_on_gpsimd(i, g, blk, tag=None):
            x_bf[i, g, blk] = sb("x_bf%d%d%d" % (i, g, blk), [P, P, T], BF16, tag=tag)[:]
            nc.gpsimd.tensor_scalar(
                out=x_bf[i, g, blk],
                in0=x_wide[i, g, blk].rearrange("p t d -> p d t"),
                scalar1=x_scale_of(i, g, blk),
                scalar2=0.0,
                op0=MULT,
                op1=ADD,
            )

        def x_quantize(i, blk):
            if (i, blk) in x_both:
                quantize(
                    x_codes[i, blk][:].rearrange("p g d -> p (g d)"),
                    x_planes[i, blk][:].rearrange("p g d -> p (g d)"),
                    x_both[i, blk][:].rearrange("p g d t -> p (g d t)"),
                )
            else:
                for g in range(2):
                    quantize(x_codes[i, blk][:, g], x_planes[i, blk][:, g], x_bf[i, g, blk].rearrange("p d t -> p (d t)"))

        def analysis(i, blk, n):
            u_ps = u_bank[i, blk] = bank(n, "u%d%d" % (i, blk))
            for t in range(T):
                for g in range(2):
                    nc.tensor.matmul_mx(
                        out=u_ps[:, cols(t)],
                        lhsT=p_codes[:, g, cols(t, 2 * P)].bitcast(E2M1),
                        lhsT_scale=p_planes[:, g, cols(t)],
                        rhs=x_codes[i, blk][:, g].bitcast(E4M3),
                        rhs_scale=x_planes[i, blk][:, g],
                        start=(g == 0),
                        stop=(g == 1),
                    )

        def keep_u(i, blk):
            u_kept[i, blk] = sb("u_kept%d%d" % (i, blk), [P, P, T], F32)
            nc.scalar.copy(out=u_kept[i, blk][:], in_=by_words(u_bank[i, blk][:]))

        q_pairs = q_raw[:].rearrange("p c j m -> p (c j m)").bitcast(F32)

        def q_turn(h, c, banks):
            for pair in range(2):
                turned = q_bank[h, c, pair] = bank(banks[pair], "turned%d%d%d" % (h, c, pair))
                for s in range(2):
                    first = (ROW_TILES * c + 4 * h + 2 * pair + s) * (M // 2)
                    for u in range(2):
                        nc.tensor.transpose(
                            turned[:, cols(2 * s + u)], q_pairs[:, first + u : first + M // 2 : 2], identity[:]
                        )

        def q_copy(h, c, pairs=range(2), copy=nc.scalar.copy):
            for pair in pairs:
                copy(
                    out=q_bf[h, c][:, cols(pair, 2)]
                    .rearrange("p s r e -> p (s r e)")
                    .bitcast(F32)
                    .rearrange("p (s r u) -> p s r u", s=2, u=2),
                    in_=q_bank[h, c, pair][:].rearrange("p (s u r) -> p s r u", s=2, u=2),
                )

        def q_quantize(h, c):
            quantize(q_codes[h, c][:], q_planes[h, c][:], q_bf[h, c][:].rearrange("p s r e -> p (s r e)"))

        def filter_part(z, n, c):
            i, blk = PIECES[z][0], PIECES[z][1] + n
            nc.vector.tensor_tensor(
                out=f_bf[z][:, c, n], in0=by_words(u_bank[i, blk][:]), in1=transfer_kept[:, blk, c], op=MULT
            )

        def filter_both(z, n):
            i, blk = PIECES[z][0], PIECES[z][1] + n
            nc.vector.tensor_tensor(
                out=f_bf[z][:, :, n],
                in0=by_words(u_bank[i, blk][:]).unsqueeze(1).to_broadcast([P, 2, P, T]),
                in1=transfer_kept[:, blk],
                op=MULT,
            )

        def filter_gpsimd(z, n, c, tag):
            i, blk = PIECES[z][0], PIECES[z][1] + n
            f_apart[z, n, c] = sb("f_apart%d%d%d" % (z, n, c), [P, P, T], BF16, tag=tag)
            nc.gpsimd.tensor_tensor(out=f_apart[z, n, c][:], in0=u_kept[i, blk][:], in1=transfer_kept[:, blk, c], op=MULT)

        def f_quantize(z, c, n=None):
            ns = slice(0, PIECES[z][2]) if n is None else slice(n, n + 1)
            ds = slice(P * ns.start, P * ns.stop)
            values = f_apart[z, n, c][:] if (z, n, c) in f_apart else f_bf[z][:, c, ns].rearrange("p n d t -> p (n d) t")
            quantize(f_codes[z][:, c, ds], f_planes[z][:, c, ds], values.rearrange("p d t -> p (d t)"))

        def synthesis(z, j0, n):
            width = P * PIECES[z][2]
            o_ps = out_bank[z, j0] = bank(n, "o%d%d" % (z, j0))
            for s in range(512 // width):
                j = j0 + s
                for c in range(2):
                    nc.tensor.matmul_mx(
                        out=o_ps[:, cols(s, width)],
                        lhsT=q_codes[j // 4, c][:, cols(j % 4)].bitcast(E4M3),
                        lhsT_scale=q_planes[j // 4, c][:, cols(j % 4)],
                        rhs=f_codes[z][:, c, :].bitcast(E4M3),
                        rhs_scale=f_planes[z][:, c, :],
                        start=(c == 0),
                        stop=(c == 1),
                    )

        def synthesis_part(z, j0, c, n=None):
            if n is not None:
                out_bank[z, j0] = bank(n, "o%d%d" % (z, j0))
            for s in range(2):
                j = j0 + s
                nc.tensor.matmul_mx(
                    out=out_bank[z, j0][:, cols(s, 2 * P)],
                    lhsT=q_codes[j // 4, c][:, cols(j % 4)].bitcast(E4M3),
                    lhsT_scale=q_planes[j // 4, c][:, cols(j % 4)],
                    rhs=f_codes[z][:, c, :].bitcast(E4M3),
                    rhs_scale=f_planes[z][:, c, :],
                    start=(n is not None and s == 0),
                    stop=(n is None and s == 1),
                )

        def copy_out(z, j0, copy=nc.scalar.copy):
            width = P * PIECES[z][2]
            copy(
                out=o_sb[z][:, j0 : j0 + 512 // width, :], in_=out_bank[z, j0][:].rearrange("p (j d) -> p j d", d=width)
            )

        def store(z, j0, tiles, queue=nc.sync):
            i, first, blocks = PIECES[z]
            rows = slice(j0, j0 + tiles)
            queue.dma_start(
                out=out[i].rearrange("(p j) d -> p j d", j=ROW_TILES)[:, rows, P * first : P * (first + blocks)],
                in_=o_sb[z][:, rows, :],
            )

        def output(z, j0, copy=nc.scalar.copy):
            copy_out(z, j0, copy)
            store(z, j0, 512 // (P * PIECES[z][2]))

        for tm in range(T):
            difference(tm, 4 + tm)
        b_ps = spread_b(0)
        scales_to_columns()
        scales_repeat()
        scales_to_rows()
        for tm in range(T):
            square(tm)
        inverse_root(0)
        inverse_root(1)
        for blk in range(BLOCKS):
            x_scale_block(0, 0, blk)
        nc.vector.tensor_copy(out=b_col[:], in_=b_ps[:, 0:T])
        for blk in range(BLOCKS):
            x_scale_block(0, 1, blk)
        x_quantize(0, 0)
        x_quantize(0, 1)
        permute_p_codes(0, nc.vector.tensor_copy)
        permute_p_codes(1, nc.vector.tensor_copy)
        permute_p_planes()
        weight_from_roots(0)
        inverse(1)
        x_quantize(0, 2)
        weight_from_inverses(1)
        g_real_gpsimd(1)
        x_quantize(0, 3)
        for tm in range(T):
            g_imaginary(tm)
        q_turn(0, 0, (1, 2))
        q_turn(0, 1, (3, 0))
        q_copy(0, 0)
        g_real_scalar(0)
        q_copy(0, 1)
        q_turn(1, 0, (1, 2))
        analysis(0, 0, 4)
        analysis(0, 1, 5)
        q_copy(1, 0)
        x_widen(1, 1, 0, 4)
        x_scale_block(1, 0, 0)
        g_quantize(1)
        g_quantize(0)
        x_scale_block(1, 0, 1)
        q_quantize(0, 0)
        q_quantize(0, 1)
        transfer(0, 1, 6)
        transfer(0, 0, 7)
        transfer(1, 1, 3)
        transfer(1, 0, 0)
        q_turn(1, 1, (1, 2))
        keep_transfer(0, 1)
        keep_transfer(0, 0)
        keep_transfer(1, 1)
        keep_transfer(1, 0)
        q_copy(1, 1)
        transfer(2, 1, 6)
        transfer(2, 0, 7)
        analysis(0, 2, 3)
        analysis(0, 3, 0)
        transfer(3, 1, 1)
        transfer(3, 0, 2)
        x_scale_on_gpsimd(1, 1, 0, "q_bf00")
        x_scale_on_gpsimd(1, 1, 1)
        filter_part(0, 0, 1)
        filter_part(0, 0, 0)
        filter_both(0, 1)
        keep_transfer(2, 1)
        keep_transfer(2, 0)
        keep_transfer(3, 1)
        keep_transfer(3, 0)
        x_quantize(1, 0)
        f_quantize(0, 1)
        f_quantize(0, 0)
        q_quantize(1, 0)
        x_quantize(1, 1)
        q_quantize(1, 1)
        synthesis(0, 0, 6)
        synthesis(0, 2, 7)
        analysis(1, 0, 4)
        analysis(1, 1, 5)
        synthesis(0, 4, 1)
        synthesis(0, 6, 2)
        x_scale_on_gpsimd(1, 1, 2, "x_bf101")
        x_scale_on_gpsimd(1, 1, 3)
        filter_both(1, 0)
        filter_both(1, 1)
        x_widen(1, 0, 2, 2)
        output(0, 0)
        x_scale_on_scalar(1, 0, 2)
        output(0, 2)
        output(0, 4)
        output(0, 6)
        x_scale_on_scalar(1, 0, 3)
        x_quantize(1, 2)
        f_quantize(1, 1)
        f_quantize(1, 0)
        analysis(1, 2, 3)
        for j, n in zip(range(0, 8, 2), (6, 7, 1, 2)):
            synthesis(1, j, n)
            output(1, j)
        filter_both(2, 0)
        filter_part(2, 1, 1)
        x_quantize(1, 3)
        analysis(1, 3, 0)
        f_quantize(2, 1)
        filter_part(2, 1, 0)
        f_quantize(2, 0, 0)
        f_quantize(2, 0, 1)
        filter_part(3, 0, 0)
        filter_part(3, 1, 0)
        filter_part(3, 0, 1)
        f_quantize(3, 0)
        filter_part(3, 1, 1)
        f_quantize(3, 1, 0)
        f_quantize(3, 1, 1)
        synthesis_part(2, 0, 1, 6)
        synthesis_part(2, 0, 0)
        output(2, 0)
        for j, n in zip(range(2, 8, 2), (7, 1, 2)):
            synthesis(2, j, n)
            output(2, j)
        synthesis_part(3, 0, 0, 4)
        synthesis_part(3, 2, 0, 5)
        synthesis_part(3, 0, 1)
        synthesis_part(3, 2, 1)
        synthesis(3, 4, 6)
        synthesis(3, 6, 7)
        output(3, 0, nc.vector.tensor_copy)
        copy_out(3, 2)
        store(3, 2, 2, nc.scalar)
        output(3, 4, nc.vector.tensor_copy)
        copy_out(3, 6)
        store(3, 6, 2, nc.scalar)
